import numpy as np
import ml_dtypes


def mxq(x, axis, fmt="e4m3"):
    dtype, down = {"e4m3": (ml_dtypes.float8_e4m3fn, 7), "e5m2": (ml_dtypes.float8_e5m2, 14)}[fmt]
    v = np.moveaxis(np.asarray(x, np.float32).astype(ml_dtypes.bfloat16).astype(np.float64), axis, -1)
    blocks = v.reshape(v.shape[:-1] + (-1, 32))
    amax = np.abs(blocks).max(-1, keepdims=True)
    byte = np.maximum(np.where(amax > 0, np.frexp(amax)[1] - 1 + 127, 0) - down, 1)
    scale = np.exp2(byte - 127.0)
    codes = (blocks / scale).astype(np.float32).astype(dtype).astype(np.float64)
    return np.moveaxis((codes * scale).reshape(v.shape), -1, axis)


WIDE = False


def mx_kscale(k):
    if not WIDE:
        return np.ones(k)
    levels = np.array([10, -10, 5, -5, 0])
    if k % 512:
        return np.exp2(np.random.permutation(np.resize(levels, k // 32))).repeat(32)
    a = np.empty((k // 512, 16))
    for p in range(k // 512):
        a[p, :8] = np.random.permutation(np.resize(levels, 8))
        for g in range(8):
            far = levels[np.abs(levels - a[p, g]) >= 10]
            a[p, g + 8] = far[np.random.randint(len(far))]
    return np.exp2(a.ravel()).repeat(32)


def f64(x):
    return np.asarray(x).astype(np.float64)


def striped(idx):
    return np.tile(idx.reshape(-1, 16).T, (8, 1)).astype(np.uint16)


def unstriped(offs):
    return offs[:16].T.reshape(-1).astype(np.int64)


def striped8(idx):
    return np.concatenate([x.reshape(-1, 16).T for x in idx]).astype(np.uint16)


def runs(offs, k):
    lists = np.stack([offs[16 * r : 16 * r + 16].T.reshape(-1) for r in range(8)]).astype(np.int64)
    return lists[np.arange(k) % 512 // 64]


def pack_weight(w):
    k, n = w.shape
    w = f64(np.asarray(w, np.float32).astype(ml_dtypes.bfloat16)).reshape(k // 32, 32, n)
    amax = np.abs(w).max(1)
    byte = np.clip(np.where(amax > 0, np.frexp(amax)[1] - 1 + 127 - 7, 1), 1, 254)
    scaled = (w * np.exp2(127.0 - byte)[:, None, :]).reshape(k, n).astype(np.float32)
    words = np.ascontiguousarray(scaled.reshape(k // 512, 128, 4, n).transpose(0, 1, 3, 2)).astype(ml_dtypes.float8_e4m3fn).view(np.uint8)
    return words, np.ascontiguousarray(byte.astype(np.uint8).reshape(k // 512, 16, n))


def unpack_weight(words, scales):
    g, p, n, _ = words.shape
    vals = np.ascontiguousarray(words).view(ml_dtypes.float8_e4m3fn).astype(np.float64) * np.repeat(np.exp2(scales.astype(np.float64) - 127.0), 8, axis=1)[..., None]
    return vals.transpose(0, 1, 3, 2).reshape(g * 512, n)

def planes(y):
    n, m = y.shape
    v = y.astype(np.float32).astype(ml_dtypes.bfloat16).astype(np.float64).reshape(n // 32, 32, m)
    top = np.abs(v).max(1)
    byte = np.clip(np.where(top > 0, np.frexp(top)[1] - 1 + 127 - 7, 1), 1, 254)
    codes = (v * np.exp2(127.0 - byte)[:, None, :]).reshape(n, m).astype(np.float32).astype(ml_dtypes.float8_e4m3fn).view(np.uint8)
    words = codes.reshape(n // 512, 128, 4, m).transpose(0, 1, 3, 2)
    return np.ascontiguousarray(words), np.ascontiguousarray(byte.astype(np.uint8).reshape(n // 512, 16, m))


K, T, S, N, U, G, H = 512, 2048, 512, 512, 1024, 2048, 512


def setup_inputs():
    n = np.random.standard_normal
    s = mx_kscale(K)[:, None]
    u = mx_kscale(H)
    packed_xT = pack_weight(n((K, T)) * s)
    packed_dT = pack_weight(n((K, G)) / s)
    packed_w1 = pack_weight(n((H, N)) / np.sqrt(H) / u[:, None])
    return {
        "x_words": packed_xT[0],
        "x_scales": packed_xT[1],
        "d_words": packed_dT[0],
        "d_scales": packed_dT[1],
        "gn": (np.random.uniform(0.5, 1.5, (H, 1)) * u[:, None]).astype(np.float32),
        "w1_words": packed_w1[0],
        "w1_scales": packed_w1[1],
        "offs": striped(np.random.permutation(T)[:S]),
        "kidx": striped8(np.random.randint(0, G, (8, H))),
        "slot": striped8(np.stack([np.random.permutation(U)[:S] for _ in range(8)])),
    }


def reference(x_words, x_scales, d_words, d_scales, gn, w1_words, w1_scales, offs, kidx, slot):
    d_kidx = unpack_weight(d_words, d_scales)[np.arange(K)[:, None], runs(kidx, K)]
    xq = unpack_weight(x_words, x_scales)[:, unstriped(offs)]
    s = np.tanh(0.0625 * (d_kidx.T @ xq))
    pt = np.zeros((H, U))
    pt[np.arange(H)[:, None], runs(slot, H)] = s
    z = f64(gn) * pt
    out_0 = unpack_weight(w1_words, w1_scales).T @ mxq(z, 0, "e4m3")
    return (out_0,) + planes(out_0)

@@ -1,0 +1,193 @@
+from contextlib import ExitStack
+
+import concourse.mybir as mybir
+
+F32 = mybir.dt.float32
+BF16 = mybir.dt.bfloat16
+I32 = mybir.dt.int32
+U32 = mybir.dt.uint32
+U16 = mybir.dt.uint16
+U8 = mybir.dt.uint8
+FP8X4 = mybir.dt.float8_e4m3fn_x4
+TANH = mybir.ActivationFunctionType.Tanh
+COPY = mybir.ActivationFunctionType.Copy
+MULT = mybir.AluOpType.mult
+
+P = 128
+PACK = 4
+TABLE = 2048
+PICKED = 512
+SLOTS = 1024
+BANK = 512
+CHUNK_WIDTHS = (128, 128, 256, 256, 128, 128)
+CHUNK_STARTS = tuple(sum(CHUNK_WIDTHS[:c]) for c in range(len(CHUNK_WIDTHS)))
+CODE_STORES_AFTER = (2, 4, 5)
+HALF = PICKED // 2
+SCORE_SCALE = 0.0625
+FLOPS = 2 * 512 * 512 * 512 + 2 * 512 * 512 * 1024
+PLANE_ORDER = (2, 0, 1, 3)
+SCALAR_CHUNKS = (3, 4)
+
+
+def as_words(dram_words):
+    return dram_words[0].rearrange("p n t -> p (n t)").bitcast(I32)
+
+
+def deal(engine, dealt, natural):
+    engine.tensor_copy(out=dealt[:].rearrange("p (t m) -> p m t", t=PACK), in_=natural[:].rearrange("p (m t) -> p m t", t=PACK))
+
+
+def tile_picked_scoreput_tanh_po_kernel(
+    tc, x_words, x_scales, d_words, d_scales, gn, w1_words, w1_scales, offs, kidx, slot, out_0, out_1, out_2
+):
+    nc = tc.nc
+    with ExitStack() as ctx:
+        keep = ctx.enter_context(tc.tile_pool(name="keep", bufs=1))
+        psum = ctx.enter_context(tc.psum_pool(name="psum", bufs=8))
+
+        kidx_sb = keep.tile([P, PICKED // 16], U16, name="kidx_sb")
+        offs_sb = keep.tile([P, PICKED // 16], U16, name="offs_sb")
+        slot_sb = keep.tile([P, PICKED // 16], U16, name="slot_sb")
+        d_table = keep.tile([P, TABLE], U32, name="d_table", align_bytes=64)
+        x_table = keep.tile([P, TABLE], U32, name="x_table", align_bytes=64)
+        d_scale_table = keep.tile([P, TABLE], U8, name="d_scale_table", align_bytes=64)
+        x_scale_table = keep.tile([P, TABLE], U8, name="x_scale_table", align_bytes=64)
+        gn_sb = keep.tile([P, PACK], F32, name="gn_sb")
+
+        nc.vector.memset(d_scale_table[:].bitcast(I32), 0)
+        nc.vector.memset(x_scale_table[:].bitcast(I32), 0)
+
+        nc.sync.dma_start(kidx_sb[:], kidx)
+        nc.sync.dma_start(offs_sb[:], offs)
+        d_rows = d_scales[0].bitcast(I32)
+        for e in range(2):
+            nc.scalar.dma_start(d_scale_table[:].bitcast(I32)[e:P:16, :], d_rows[e:16:2, :])
+        nc.sync.dma_start(d_table[:].bitcast(I32), as_words(d_words))
+        x_rows = x_scales[0].bitcast(I32)
+        for r in range(4):
+            nc.scalar.dma_start(x_scale_table[:].bitcast(I32)[r:P:32, :], x_rows[r:16:4, :])
+        nc.sync.dma_start(x_table[:].bitcast(I32), as_words(x_words))
+        nc.sync.dma_start(slot_sb[:], slot)
+        nc.sync.dma_start(gn_sb[:], gn.rearrange("(p t) o -> p (t o)", t=PACK))
+
+        windows = [keep.tile([P, SLOTS], F32, name="window%d" % t) for t in range(PACK)]
+        for t in PLANE_ORDER:
+            nc.vector.memset(windows[t][:], 0.0)
+
+        d_scale_picked = keep.tile([P, PICKED], U8, name="d_scale_picked", tag="picked_bytes", align_bytes=64)
+        d_scale_dealt = keep.tile([P, PICKED], U8, name="d_scale_dealt", align_bytes=64)
+        nc.vector.tensor_copy(d_scale_picked[:], d_scale_table[:].indirect(kidx_sb[:]))
+        deal(nc.vector, d_scale_dealt, d_scale_picked)
+        for e in range(2):
+            nc.scalar.dma_start(d_scale_dealt[:].bitcast(I32)[2 + e : P : 32, :], d_scale_dealt[:].bitcast(I32)[16 + e : P : 32, :])
+
+        d_picked = keep.tile([P, PICKED], U32, name="d_picked", tag="picked_words", align_bytes=64)
+        d_dealt = keep.tile([P, PICKED], U32, name="d_dealt", align_bytes=64)
+        nc.vector.tensor_copy(d_picked[:], d_table[:].indirect(kidx_sb[:]))
+        deal(nc.vector, d_dealt, d_picked)
+
+        x_scale_picked = keep.tile([P, PICKED], U8, name="x_scale_picked", align_bytes=64)
+        x_picked = keep.tile([P, PICKED], U32, name="x_picked", align_bytes=64)
+        nc.vector.tensor_copy(x_scale_picked[:], x_scale_table[:].indirect(offs_sb[:]))
+        for h in range(2):
+            nc.vector.tensor_copy(x_picked[:, h * HALF : (h + 1) * HALF], x_table[:].indirect(offs_sb[:, h * 16 : (h + 1) * 16]))
+
+        w_natural = keep.tile([P, PICKED], U32, name="w_natural", tag="picked_words", align_bytes=64)
+        w_scale_natural = keep.tile([P, PICKED], U8, name="w_scale_natural", tag="picked_bytes", align_bytes=64)
+        w_dealt = keep.tile([P, PICKED], U32, name="w_dealt", align_bytes=64)
+        w_scale_dealt = keep.tile([P, PICKED], U8, name="w_scale_dealt", align_bytes=64)
+        nc.sync.dma_start(w_natural[:].bitcast(I32), as_words(w1_words))
+        nc.gpsimd.memset(w_scale_natural[:], 0)
+        w_rows = w1_scales[0].bitcast(I32)
+        for r in range(4):
+            nc.sync.dma_start(w_scale_natural[:].bitcast(I32)[r:P:32, :], w_rows[r:16:4, :])
+        deal(nc.gpsimd, w_dealt, w_natural)
+        deal(nc.gpsimd, w_scale_dealt, w_scale_natural)
+
+        z = keep.tile([P, SLOTS, PACK], BF16, name="z", align_bytes=64)
+        first_plane, last_plane = PLANE_ORDER[0], PLANE_ORDER[-1]
+        first_weight = keep.tile([P, 1], F32, name="first_weight", tag="pair_weight")
+        nc.scalar.copy(out=first_weight[:], in_=gn_sb[:, first_plane : first_plane + 1])
+
+        def weigh(t, cols, weight, on_scalar):
+            if on_scalar:
+                nc.scalar.activation(out=z[:, cols, t], in_=windows[t][:, cols], func=COPY, scale=weight)
+            else:
+                nc.vector.tensor_scalar(z[:, cols, t], windows[t][:, cols], weight, None, MULT)
+
+        scores = [keep.tile([P, PICKED], F32, name="scores%d" % t) for t in range(PACK)]
+        pieces = []
+        for t in PLANE_ORDER:
+            width = HALF if t == PLANE_ORDER[0] else PICKED
+            for j0 in range(0, PICKED, width):
+                pieces.append((t, j0, width))
+        for t, j0, width in pieces:
+            keys = slice(t * P, (t + 1) * P)
+            tokens = slice(j0, j0 + width)
+            bank = psum.tile([P, BANK], F32, name="bank", tag="bank")
+            nc.tensor.matmul_mx(
+                out=bank[:, 0:width],
+                lhsT=d_dealt[:, keys].bitcast(FP8X4),
+                lhsT_scale=d_scale_dealt[:, keys],
+                rhs=x_picked[:, tokens].bitcast(FP8X4),
+                rhs_scale=x_scale_picked[:, tokens],
+                start=True,
+                stop=True,
+            )
+            nc.scalar.activation(out=scores[t][:, tokens], in_=bank[:, 0:width], func=TANH, scale=SCORE_SCALE)
+        for t, j0, width in pieces:
+            entries = slot_sb[:, j0 // 16 : (j0 + width) // 16]
+            nc.vector.tensor_copy(windows[t][:].indirect(entries), scores[t][:, j0 : j0 + width])
+            if j0 + width == PICKED and t != PLANE_ORDER[-1]:
+                weight = first_weight[:] if t == first_plane else gn_sb[:, t : t + 1]
+                for w0 in range(0, SLOTS, SLOTS // 2):
+                    weigh(t, slice(w0, w0 + SLOTS // 2), weight, True)
+
+        last_weight = keep.tile([P, 1], F32, name="last_weight", tag="pair_weight")
+        nc.scalar.copy(out=last_weight[:], in_=gn_sb[:, last_plane : last_plane + 1])
+        z_codes = keep.tile([P, SLOTS], U32, name="z_codes", align_bytes=64)
+        z_scales = keep.tile([P, SLOTS], U8, name="z_scales", align_bytes=64)
+        chunks = [slice(w0, w0 + width) for w0, width in zip(CHUNK_STARTS, CHUNK_WIDTHS)]
+        for c, cols in enumerate(chunks):
+            weigh(last_plane, cols, last_weight[:], c in SCALAR_CHUNKS)
+            nc.vector.quantize_mx(out=z_codes[:, cols].bitcast(FP8X4), scales=z_scales[:, cols], in_=z[:, cols, :].rearrange("p w t -> p (w t)"))
+
+        y_codes = keep.tile([P, SLOTS], U32, name="y_codes", align_bytes=64)
+        y_scales = keep.tile([P, SLOTS], U8, name="y_scales", align_bytes=64)
+        out_rows = out_0.rearrange("(p t) w -> p t w", t=PACK)
+        out_words = as_words(out_1)
+        stored = 0
+        for c, cols in enumerate(chunks):
+            width = CHUNK_WIDTHS[c]
+            per_bank = BANK // width
+            y = keep.tile([P, PACK, width], F32, name="y%d" % c)
+            for t0 in range(0, PACK, per_bank):
+                bank = psum.tile([P, BANK], F32, name="bank", tag="bank")
+                for j in range(per_bank):
+                    rows = slice((t0 + j) * P, (t0 + j + 1) * P)
+                    nc.tensor.matmul_mx(
+                        out=bank[:, j * width : (j + 1) * width],
+                        lhsT=w_dealt[:, rows].bitcast(FP8X4),
+                        lhsT_scale=w_scale_dealt[:, rows],
+                        rhs=z_codes[:, cols].bitcast(FP8X4),
+                        rhs_scale=z_scales[:, cols],
+                        start=True,
+                        stop=True,
+                    )
+                planes = slice(t0, t0 + per_bank)
+                nc.scalar.copy(out=y[:, planes, :].rearrange("p t w -> p (t w)"), in_=bank[:])
+                nc.sync.dma_start(out_rows[:, planes, cols], y[:, planes, :])
+            y_rounded = keep.tile([P, width, PACK], BF16, name="y_rounded%d" % c, align_bytes=64)
+            nc.vector.tensor_copy(
+                out=y_rounded[:].rearrange("p (b i) t -> p b t i", i=4),
+                in_=y[:].rearrange("p t (b i) -> p b t i", i=4),
+            )
+            nc.vector.quantize_mx(out=y_codes[:, cols].bitcast(FP8X4), scales=y_scales[:, cols], in_=y_rounded[:].rearrange("p w t -> p (w t)"))
+            if c in CODE_STORES_AFTER:
+                done = slice(stored, cols.stop)
+                nc.sync.dma_start(out_words[:, done], y_codes[:, done].bitcast(I32))
+                stored = cols.stop
+        out_scale_rows = out_2[0].bitcast(I32)
+        for r in range(4):
+            queue = nc.sync if r == 3 else nc.scalar
+            queue.dma_start(out_scale_rows[r:16:4, :], y_scales[:].bitcast(I32)[r:P:32, :])

@@ -25,8 +25,9 @@ CODE_STORES_AFTER = (2, 4, 5)
 HALF = PICKED // 2
 SCORE_SCALE = 0.0625
 FLOPS = 2 * 512 * 512 * 512 + 2 * 512 * 512 * 1024
-PLANE_ORDER = (2, 0, 1, 3)
+PLANE_ORDER = (0, 1, 2, 3)
 SCALAR_CHUNKS = (3, 4)
+PARTNER_SPANS = (((0, 256),), ((256, 1024),))
 
 
 def as_words(dram_words):
@@ -49,65 +50,68 @@ def tile_picked_scoreput_tanh_po_kernel(
         offs_sb = keep.tile([P, PICKED // 16], U16, name="offs_sb")
         slot_sb = keep.tile([P, PICKED // 16], U16, name="slot_sb")
         d_table = keep.tile([P, TABLE], U32, name="d_table", align_bytes=64)
-        x_table = keep.tile([P, TABLE], U32, name="x_table", align_bytes=64)
+        x_table = keep.tile([P, TABLE], U32, name="x_table", tag="x_table", align_bytes=64)
         d_scale_table = keep.tile([P, TABLE], U8, name="d_scale_table", align_bytes=64)
         x_scale_table = keep.tile([P, TABLE], U8, name="x_scale_table", align_bytes=64)
         gn_sb = keep.tile([P, PACK], F32, name="gn_sb")
 
-        nc.vector.memset(d_scale_table[:].bitcast(I32), 0)
-        nc.vector.memset(x_scale_table[:].bitcast(I32), 0)
+        w_natural = keep.tile([P, PICKED], U32, name="w_natural", align_bytes=64)
+        nc.gpsimd.memset(d_scale_table[:].bitcast(I32), 0)
+        nc.gpsimd.memset(x_scale_table[:].bitcast(I32), 0)
 
+        d_source = as_words(d_words)
+        d_rows = d_scales[0].bitcast(I32)
+        x_rows = x_scales[0].bitcast(I32)
         nc.sync.dma_start(kidx_sb[:], kidx)
         nc.sync.dma_start(offs_sb[:], offs)
-        d_rows = d_scales[0].bitcast(I32)
-        for e in range(2):
-            nc.scalar.dma_start(d_scale_table[:].bitcast(I32)[e:P:16, :], d_rows[e:16:2, :])
-        nc.sync.dma_start(d_table[:].bitcast(I32), as_words(d_words))
-        x_rows = x_scales[0].bitcast(I32)
+        nc.sync.dma_start(d_table[:].bitcast(I32)[:, : TABLE // 2], d_source[:, : TABLE // 2])
+        nc.sync.dma_start(d_scale_table[:].bitcast(I32)[0:P:8, :], d_rows)
+        nc.sync.dma_start(d_table[:].bitcast(I32)[:, TABLE // 2 :], d_source[:, TABLE // 2 :])
         for r in range(4):
-            nc.scalar.dma_start(x_scale_table[:].bitcast(I32)[r:P:32, :], x_rows[r:16:4, :])
+            nc.sync.dma_start(x_scale_table[:].bitcast(I32)[r:P:32, :], x_rows[r:16:4, :])
         nc.sync.dma_start(x_table[:].bitcast(I32), as_words(x_words))
         nc.sync.dma_start(slot_sb[:], slot)
-        nc.sync.dma_start(gn_sb[:], gn.rearrange("(p t) o -> p (t o)", t=PACK))
 
         windows = [keep.tile([P, SLOTS], F32, name="window%d" % t) for t in range(PACK)]
         for t in PLANE_ORDER:
-            nc.vector.memset(windows[t][:], 0.0)
+            engine = nc.vector if t < 2 else nc.gpsimd
+            engine.memset(windows[t][:], 0.0)
+        nc.gpsimd.dma_start(gn_sb[:], gn.rearrange("(p t) o -> p (t o)", t=PACK))
+        nc.gpsimd.dma_start(w_natural[:].bitcast(I32), as_words(w1_words))
 
         d_scale_picked = keep.tile([P, PICKED], U8, name="d_scale_picked", tag="picked_bytes", align_bytes=64)
         d_scale_dealt = keep.tile([P, PICKED], U8, name="d_scale_dealt", align_bytes=64)
         nc.vector.tensor_copy(d_scale_picked[:], d_scale_table[:].indirect(kidx_sb[:]))
         deal(nc.vector, d_scale_dealt, d_scale_picked)
-        for e in range(2):
-            nc.scalar.dma_start(d_scale_dealt[:].bitcast(I32)[2 + e : P : 32, :], d_scale_dealt[:].bitcast(I32)[16 + e : P : 32, :])
+        for r in range(1, 4):
+            nc.scalar.dma_start(d_scale_dealt[:].bitcast(I32)[r:P:32, :], d_scale_dealt[:].bitcast(I32)[8 * r : P : 32, :])
 
-        d_picked = keep.tile([P, PICKED], U32, name="d_picked", tag="picked_words", align_bytes=64)
+        d_picked = keep.tile([P, PICKED], U32, name="d_picked", align_bytes=64)
         d_dealt = keep.tile([P, PICKED], U32, name="d_dealt", align_bytes=64)
         nc.vector.tensor_copy(d_picked[:], d_table[:].indirect(kidx_sb[:]))
         deal(nc.vector, d_dealt, d_picked)
 
         x_scale_picked = keep.tile([P, PICKED], U8, name="x_scale_picked", align_bytes=64)
-        x_picked = keep.tile([P, PICKED], U32, name="x_picked", align_bytes=64)
+        x_picked = [keep.tile([P, HALF], U32, name="x_picked%d" % h, align_bytes=64) for h in range(2)]
         nc.vector.tensor_copy(x_scale_picked[:], x_scale_table[:].indirect(offs_sb[:]))
         for h in range(2):
-            nc.vector.tensor_copy(x_picked[:, h * HALF : (h + 1) * HALF], x_table[:].indirect(offs_sb[:, h * 16 : (h + 1) * 16]))
+            nc.vector.tensor_copy(x_picked[h][:], x_table[:].indirect(offs_sb[:, h * 16 : (h + 1) * 16]))
 
-        w_natural = keep.tile([P, PICKED], U32, name="w_natural", tag="picked_words", align_bytes=64)
+        w_dealt = keep.tile([P, PICKED], U32, name="w_dealt", tag="x_table", align_bytes=64)
+        deal(nc.vector, w_dealt, w_natural)
         w_scale_natural = keep.tile([P, PICKED], U8, name="w_scale_natural", tag="picked_bytes", align_bytes=64)
-        w_dealt = keep.tile([P, PICKED], U32, name="w_dealt", align_bytes=64)
-        w_scale_dealt = keep.tile([P, PICKED], U8, name="w_scale_dealt", align_bytes=64)
-        nc.sync.dma_start(w_natural[:].bitcast(I32), as_words(w1_words))
-        nc.gpsimd.memset(w_scale_natural[:], 0)
+        nc.gpsimd.memset(w_scale_natural[:].bitcast(I32), 0)
         w_rows = w1_scales[0].bitcast(I32)
         for r in range(4):
             nc.sync.dma_start(w_scale_natural[:].bitcast(I32)[r:P:32, :], w_rows[r:16:4, :])
-        deal(nc.gpsimd, w_dealt, w_natural)
-        deal(nc.gpsimd, w_scale_dealt, w_scale_natural)
 
         z = keep.tile([P, SLOTS, PACK], BF16, name="z", align_bytes=64)
-        first_plane, last_plane = PLANE_ORDER[0], PLANE_ORDER[-1]
-        first_weight = keep.tile([P, 1], F32, name="first_weight", tag="pair_weight")
-        nc.scalar.copy(out=first_weight[:], in_=gn_sb[:, first_plane : first_plane + 1])
+        partner_plane, last_plane = PLANE_ORDER[-2], PLANE_ORDER[-1]
+        partner_weight, last_weight = [], []
+        for h in range(2):
+            weight = keep.tile([P, 1], F32, name="partner_weight%d" % h, tag="pair_weight%d" % h)
+            nc.gpsimd.tensor_copy(out=weight[:], in_=gn_sb[:, partner_plane : partner_plane + 1])
+            partner_weight.append(weight)
 
         def weigh(t, cols, weight, on_scalar):
             if on_scalar:
@@ -115,7 +119,7 @@ def tile_picked_scoreput_tanh_po_kernel(
             else:
                 nc.vector.tensor_scalar(z[:, cols, t], windows[t][:, cols], weight, None, MULT)
 
-        scores = [keep.tile([P, PICKED], F32, name="scores%d" % t) for t in range(PACK)]
+        scores = []
         pieces = []
         for t in PLANE_ORDER:
             width = HALF if t == PLANE_ORDER[0] else PICKED
@@ -123,33 +127,45 @@ def tile_picked_scoreput_tanh_po_kernel(
                 pieces.append((t, j0, width))
         for t, j0, width in pieces:
             keys = slice(t * P, (t + 1) * P)
-            tokens = slice(j0, j0 + width)
             bank = psum.tile([P, BANK], F32, name="bank", tag="bank")
-            nc.tensor.matmul_mx(
-                out=bank[:, 0:width],
-                lhsT=d_dealt[:, keys].bitcast(FP8X4),
-                lhsT_scale=d_scale_dealt[:, keys],
-                rhs=x_picked[:, tokens].bitcast(FP8X4),
-                rhs_scale=x_scale_picked[:, tokens],
-                start=True,
-                stop=True,
-            )
-            nc.scalar.activation(out=scores[t][:, tokens], in_=bank[:, 0:width], func=TANH, scale=SCORE_SCALE)
-        for t, j0, width in pieces:
+            for j in range(j0, j0 + width, HALF):
+                nc.tensor.matmul_mx(
+                    out=bank[:, j - j0 : j - j0 + HALF],
+                    lhsT=d_dealt[:, keys].bitcast(FP8X4),
+                    lhsT_scale=d_scale_dealt[:, keys],
+                    rhs=x_picked[j // HALF][:].bitcast(FP8X4),
+                    rhs_scale=x_scale_picked[:, j : j + HALF],
+                    start=True,
+                    stop=True,
+                )
+            piece_scores = keep.tile([P, width], F32, name="scores%d_%d" % (t, j0), tag="scores%d_%d" % (t, j0), align_bytes=64)
+            scores.append(piece_scores)
+            nc.scalar.activation(out=piece_scores[:], in_=bank[:, 0:width], func=TANH, scale=SCORE_SCALE)
+        for (t, j0, width), piece_scores in zip(pieces, scores):
             entries = slot_sb[:, j0 // 16 : (j0 + width) // 16]
-            nc.vector.tensor_copy(windows[t][:].indirect(entries), scores[t][:, j0 : j0 + width])
+            nc.vector.tensor_copy(windows[t][:].indirect(entries), piece_scores[:])
+            if t == PLANE_ORDER[0] and j0 == 0:
+                w_scale_dealt = keep.tile([P, PICKED], U8, name="w_scale_dealt", tag="scores%d_0" % t, align_bytes=64)
+                deal(nc.vector, w_scale_dealt, w_scale_natural)
             if j0 + width == PICKED and t != PLANE_ORDER[-1]:
-                weight = first_weight[:] if t == first_plane else gn_sb[:, t : t + 1]
-                for w0 in range(0, SLOTS, SLOTS // 2):
-                    weigh(t, slice(w0, w0 + SLOTS // 2), weight, True)
+                if t != partner_plane:
+                    weigh(t, slice(0, SLOTS), gn_sb[:, t : t + 1], True)
+                    continue
+                for h, spans in enumerate(PARTNER_SPANS):
+                    for w0, w1 in spans:
+                        weigh(t, slice(w0, w1), partner_weight[h][:], True)
+                    weight = keep.tile([P, 1], F32, name="last_weight%d" % h, tag="pair_weight%d" % h)
+                    nc.gpsimd.tensor_copy(out=weight[:], in_=gn_sb[:, last_plane : last_plane + 1])
+                    last_weight.append(weight)
 
-        last_weight = keep.tile([P, 1], F32, name="last_weight", tag="pair_weight")
-        nc.scalar.copy(out=last_weight[:], in_=gn_sb[:, last_plane : last_plane + 1])
         z_codes = keep.tile([P, SLOTS], U32, name="z_codes", align_bytes=64)
         z_scales = keep.tile([P, SLOTS], U8, name="z_scales", align_bytes=64)
         chunks = [slice(w0, w0 + width) for w0, width in zip(CHUNK_STARTS, CHUNK_WIDTHS)]
         for c, cols in enumerate(chunks):
-            weigh(last_plane, cols, last_weight[:], c in SCALAR_CHUNKS)
+            if c in SCALAR_CHUNKS:
+                weigh(last_plane, cols, gn_sb[:, last_plane : last_plane + 1], True)
+            else:
+                weigh(last_plane, cols, last_weight[0 if c < 2 else 1][:], False)
             nc.vector.quantize_mx(out=z_codes[:, cols].bitcast(FP8X4), scales=z_scales[:, cols], in_=z[:, cols, :].rearrange("p w t -> p (w t)"))
 
         y_codes = keep.tile([P, SLOTS], U32, name="y_codes", align_bytes=64)

@@ -12,6 +12,7 @@ FP8X4 = mybir.dt.float8_e4m3fn_x4
 TANH = mybir.ActivationFunctionType.Tanh
 COPY = mybir.ActivationFunctionType.Copy
 MULT = mybir.AluOpType.mult
+ADD = mybir.AluOpType.add
 
 P = 128
 PACK = 4
@@ -25,9 +26,11 @@ CODE_STORES_AFTER = (2, 4, 5)
 HALF = PICKED // 2
 SCORE_SCALE = 0.0625
 FLOPS = 2 * 512 * 512 * 512 + 2 * 512 * 512 * 1024
-PLANE_ORDER = (0, 1, 2, 3)
+PLANE_ORDER = (2, 0, 1, 3)
 SCALAR_CHUNKS = (3, 4)
-PARTNER_SPANS = (((0, 256),), ((256, 1024),))
+EARLY_SLOTS = 256
+GPSIMD_FROM = 896
+FIRST_COLUMNS = 512
 
 
 def as_words(dram_words):
@@ -64,36 +67,37 @@ def tile_picked_scoreput_tanh_po_kernel(
         x_rows = x_scales[0].bitcast(I32)
         nc.sync.dma_start(kidx_sb[:], kidx)
         nc.sync.dma_start(offs_sb[:], offs)
-        nc.sync.dma_start(d_table[:].bitcast(I32)[:, : TABLE // 2], d_source[:, : TABLE // 2])
+        nc.sync.dma_start(d_table[:].bitcast(I32)[:, :FIRST_COLUMNS], d_source[:, :FIRST_COLUMNS])
         nc.sync.dma_start(d_scale_table[:].bitcast(I32)[0:P:8, :], d_rows)
-        nc.sync.dma_start(d_table[:].bitcast(I32)[:, TABLE // 2 :], d_source[:, TABLE // 2 :])
+        nc.sync.dma_start(d_table[:].bitcast(I32)[:, FIRST_COLUMNS:], d_source[:, FIRST_COLUMNS:])
         for r in range(4):
             nc.sync.dma_start(x_scale_table[:].bitcast(I32)[r:P:32, :], x_rows[r:16:4, :])
         nc.sync.dma_start(x_table[:].bitcast(I32), as_words(x_words))
         nc.sync.dma_start(slot_sb[:], slot)
 
-        windows = [keep.tile([P, SLOTS], F32, name="window%d" % t) for t in range(PACK)]
-        for t in PLANE_ORDER:
-            engine = nc.vector if t < 2 else nc.gpsimd
-            engine.memset(windows[t][:], 0.0)
-        nc.gpsimd.dma_start(gn_sb[:], gn.rearrange("(p t) o -> p (t o)", t=PACK))
         nc.gpsimd.dma_start(w_natural[:].bitcast(I32), as_words(w1_words))
+        nc.gpsimd.dma_start(gn_sb[:], gn.rearrange("(p t) o -> p (t o)", t=PACK))
+        windows = {}
+        for t in PLANE_ORDER[:2]:
+            windows[t] = keep.tile([P, SLOTS], F32, name="window%d" % t)
+            nc.vector.memset(windows[t][:], 0.0)
 
         d_scale_picked = keep.tile([P, PICKED], U8, name="d_scale_picked", tag="picked_bytes", align_bytes=64)
         d_scale_dealt = keep.tile([P, PICKED], U8, name="d_scale_dealt", align_bytes=64)
         nc.vector.tensor_copy(d_scale_picked[:], d_scale_table[:].indirect(kidx_sb[:]))
         deal(nc.vector, d_scale_dealt, d_scale_picked)
         for r in range(1, 4):
-            nc.scalar.dma_start(d_scale_dealt[:].bitcast(I32)[r:P:32, :], d_scale_dealt[:].bitcast(I32)[8 * r : P : 32, :])
+            queue = nc.sync if r == 2 else nc.scalar
+            queue.dma_start(d_scale_dealt[:].bitcast(I32)[r:P:32, :], d_scale_dealt[:].bitcast(I32)[8 * r : P : 32, :])
 
         d_picked = keep.tile([P, PICKED], U32, name="d_picked", align_bytes=64)
         d_dealt = keep.tile([P, PICKED], U32, name="d_dealt", align_bytes=64)
         nc.vector.tensor_copy(d_picked[:], d_table[:].indirect(kidx_sb[:]))
-        deal(nc.vector, d_dealt, d_picked)
 
         x_scale_picked = keep.tile([P, PICKED], U8, name="x_scale_picked", align_bytes=64)
         x_picked = [keep.tile([P, HALF], U32, name="x_picked%d" % h, align_bytes=64) for h in range(2)]
         nc.vector.tensor_copy(x_scale_picked[:], x_scale_table[:].indirect(offs_sb[:]))
+        deal(nc.vector, d_dealt, d_picked)
         for h in range(2):
             nc.vector.tensor_copy(x_picked[h][:], x_table[:].indirect(offs_sb[:, h * 16 : (h + 1) * 16]))
 
@@ -105,19 +109,26 @@ def tile_picked_scoreput_tanh_po_kernel(
         for r in range(4):
             nc.sync.dma_start(w_scale_natural[:].bitcast(I32)[r:P:32, :], w_rows[r:16:4, :])
 
-        z = keep.tile([P, SLOTS, PACK], BF16, name="z", align_bytes=64)
-        partner_plane, last_plane = PLANE_ORDER[-2], PLANE_ORDER[-1]
-        partner_weight, last_weight = [], []
-        for h in range(2):
-            weight = keep.tile([P, 1], F32, name="partner_weight%d" % h, tag="pair_weight%d" % h)
-            nc.gpsimd.tensor_copy(out=weight[:], in_=gn_sb[:, partner_plane : partner_plane + 1])
-            partner_weight.append(weight)
+        w_scale_dealt = keep.tile([P, PICKED], U8, name="w_scale_dealt", align_bytes=64)
+        deal(nc.gpsimd, w_scale_dealt, w_scale_natural)
 
-        def weigh(t, cols, weight, on_scalar):
-            if on_scalar:
+        z = keep.tile([P, SLOTS, PACK], BF16, name="z", align_bytes=64)
+        last_plane = PLANE_ORDER[-1]
+        held_weight = {}
+        for t in (PLANE_ORDER[0], PLANE_ORDER[2]):
+            held_weight[t] = keep.tile([P, 1], F32, name="held_weight%d" % t, tag="weight%d" % t)
+            nc.gpsimd.tensor_copy(out=held_weight[t][:], in_=gn_sb[:, t : t + 1])
+        last_weight = []
+        scalar_weight = keep.tile([P, 1], F32, name="scalar_weight", tag="y0")
+        nc.gpsimd.tensor_copy(out=scalar_weight[:], in_=gn_sb[:, last_plane : last_plane + 1])
+
+        def weigh(t, cols, weight, engine):
+            if engine == "scalar":
                 nc.scalar.activation(out=z[:, cols, t], in_=windows[t][:, cols], func=COPY, scale=weight)
-            else:
+            elif engine == "vector":
                 nc.vector.tensor_scalar(z[:, cols, t], windows[t][:, cols], weight, None, MULT)
+            else:
+                nc.gpsimd.tensor_scalar(z[:, cols, t], windows[t][:, cols], weight, 0.0, MULT, ADD)
 
         scores = []
         pieces = []
@@ -144,18 +155,22 @@ def tile_picked_scoreput_tanh_po_kernel(
         for (t, j0, width), piece_scores in zip(pieces, scores):
             entries = slot_sb[:, j0 // 16 : (j0 + width) // 16]
             nc.vector.tensor_copy(windows[t][:].indirect(entries), piece_scores[:])
-            if t == PLANE_ORDER[0] and j0 == 0:
-                w_scale_dealt = keep.tile([P, PICKED], U8, name="w_scale_dealt", tag="scores%d_0" % t, align_bytes=64)
-                deal(nc.vector, w_scale_dealt, w_scale_natural)
             if j0 + width == PICKED and t != PLANE_ORDER[-1]:
-                if t != partner_plane:
-                    weigh(t, slice(0, SLOTS), gn_sb[:, t : t + 1], True)
-                    continue
-                for h, spans in enumerate(PARTNER_SPANS):
-                    for w0, w1 in spans:
-                        weigh(t, slice(w0, w1), partner_weight[h][:], True)
-                    weight = keep.tile([P, 1], F32, name="last_weight%d" % h, tag="pair_weight%d" % h)
-                    nc.gpsimd.tensor_copy(out=weight[:], in_=gn_sb[:, last_plane : last_plane + 1])
+                place = PLANE_ORDER.index(t)
+                plain = gn_sb[:, t : t + 1]
+                if place == 2:
+                    weigh(t, slice(0, EARLY_SLOTS), plain, "scalar")
+                    weigh(t, slice(EARLY_SLOTS, GPSIMD_FROM), plain, "scalar")
+                else:
+                    weigh(t, slice(0, GPSIMD_FROM), held_weight[t][:] if place == 0 else plain, "scalar")
+                weigh(t, slice(GPSIMD_FROM, SLOTS), held_weight[t][:] if place == 2 else plain, "gpsimd")
+                if place < 2:
+                    later = PLANE_ORDER[place + 2]
+                    windows[later] = keep.tile([P, SLOTS], F32, name="window%d" % later, tag="scores%d_%d" % (t, j0), align_bytes=64)
+                    nc.gpsimd.memset(windows[later][:], 0.0)
+                if t in held_weight:
+                    weight = keep.tile([P, 1], F32, name="last_weight%d" % t, tag="weight%d" % t)
+                    nc.scalar.copy(out=weight[:], in_=gn_sb[:, last_plane : last_plane + 1])
                     last_weight.append(weight)
 
         z_codes = keep.tile([P, SLOTS], U32, name="z_codes", align_bytes=64)
@@ -163,20 +178,28 @@ def tile_picked_scoreput_tanh_po_kernel(
         chunks = [slice(w0, w0 + width) for w0, width in zip(CHUNK_STARTS, CHUNK_WIDTHS)]
         for c, cols in enumerate(chunks):
             if c in SCALAR_CHUNKS:
-                weigh(last_plane, cols, gn_sb[:, last_plane : last_plane + 1], True)
+                weight = scalar_weight[:]
             else:
-                weigh(last_plane, cols, last_weight[0 if c < 2 else 1][:], False)
-            nc.vector.quantize_mx(out=z_codes[:, cols].bitcast(FP8X4), scales=z_scales[:, cols], in_=z[:, cols, :].rearrange("p w t -> p (w t)"))
+                weight = last_weight[0 if cols.start < EARLY_SLOTS else 1][:]
+            weigh(last_plane, cols, weight, "scalar" if c in SCALAR_CHUNKS else "vector")
+            if c != len(chunks) - 2:
+                span = slice(chunks[c - 1].start, cols.stop) if c == len(chunks) - 1 else cols
+                nc.vector.quantize_mx(out=z_codes[:, span].bitcast(FP8X4), scales=z_scales[:, span], in_=z[:, span, :].rearrange("p w t -> p (w t)"))
 
         y_codes = keep.tile([P, SLOTS], U32, name="y_codes", align_bytes=64)
         y_scales = keep.tile([P, SLOTS], U8, name="y_scales", align_bytes=64)
         out_rows = out_0.rearrange("(p t) w -> p t w", t=PACK)
         out_words = as_words(out_1)
         stored = 0
+        y_rounded = keep.tile([P, SLOTS, PACK], BF16, name="y_rounded", align_bytes=64)
         for c, cols in enumerate(chunks):
             width = CHUNK_WIDTHS[c]
             per_bank = BANK // width
-            y = keep.tile([P, PACK, width], F32, name="y%d" % c)
+            if c != len(chunks) - 1:
+                stored_width = 2 * width if c == len(chunks) - 2 else width
+                y_tile = keep.tile([P, PACK, stored_width], F32, name="y%d" % c, tag="y%d" % c)
+                y_start = cols.start
+            y = y_tile[:, :, cols.start - y_start : cols.stop - y_start]
             for t0 in range(0, PACK, per_bank):
                 bank = psum.tile([P, BANK], F32, name="bank", tag="bank")
                 for j in range(per_bank):
@@ -191,19 +214,21 @@ def tile_picked_scoreput_tanh_po_kernel(
                         stop=True,
                     )
                 planes = slice(t0, t0 + per_bank)
-                nc.scalar.copy(out=y[:, planes, :].rearrange("p t w -> p (t w)"), in_=bank[:])
-                nc.sync.dma_start(out_rows[:, planes, cols], y[:, planes, :])
-            y_rounded = keep.tile([P, width, PACK], BF16, name="y_rounded%d" % c, align_bytes=64)
+                nc.scalar.copy(out=y[:, planes, :], in_=bank[:].rearrange("p (t w) -> p t w", t=per_bank))
+                if c != len(chunks) - 2:
+                    nc.sync.dma_start(out_rows[:, planes, y_start : cols.stop], y_tile[:, planes, :])
             nc.vector.tensor_copy(
-                out=y_rounded[:].rearrange("p (b i) t -> p b t i", i=4),
-                in_=y[:].rearrange("p t (b i) -> p b t i", i=4),
+                out=y_rounded[:, cols, :].rearrange("p (b i) t -> p b t i", i=4),
+                in_=y.rearrange("p t (b i) -> p b t i", i=4),
             )
-            nc.vector.quantize_mx(out=y_codes[:, cols].bitcast(FP8X4), scales=y_scales[:, cols], in_=y_rounded[:].rearrange("p w t -> p (w t)"))
+            if c != 0:
+                span = slice(0, cols.stop) if c == 1 else cols
+                nc.vector.quantize_mx(out=y_codes[:, span].bitcast(FP8X4), scales=y_scales[:, span], in_=y_rounded[:, span, :].rearrange("p w t -> p (w t)"))
             if c in CODE_STORES_AFTER:
                 done = slice(stored, cols.stop)
                 nc.sync.dma_start(out_words[:, done], y_codes[:, done].bitcast(I32))
                 stored = cols.stop
         out_scale_rows = out_2[0].bitcast(I32)
         for r in range(4):
-            queue = nc.sync if r == 3 else nc.scalar
+            queue = nc.sync if r >= 2 else nc.scalar
             queue.dma_start(out_scale_rows[r:16:4, :], y_scales[:].bitcast(I32)[r:P:32, :])

@@ -20,17 +20,16 @@ TABLE = 2048
 PICKED = 512
 SLOTS = 1024
 BANK = 512
-CHUNK_WIDTHS = (128, 128, 256, 256, 128, 128)
-CHUNK_STARTS = tuple(sum(CHUNK_WIDTHS[:c]) for c in range(len(CHUNK_WIDTHS)))
-CODE_STORES_AFTER = (2, 4, 5)
 HALF = PICKED // 2
 SCORE_SCALE = 0.0625
 FLOPS = 2 * 512 * 512 * 512 + 2 * 512 * 512 * 1024
-PLANE_ORDER = (2, 0, 1, 3)
-SCALAR_CHUNKS = (3, 4)
-EARLY_SLOTS = 256
-GPSIMD_FROM = 896
+PART_ORDER = (2, 0, 1, 3)
+UPPER_FROM = 768
 FIRST_COLUMNS = 512
+SCALAR_FROM = 640
+CHUNK_WIDTHS = (128, 128, 256, 512)
+VECTOR_BANK = 6
+PLANE_WIDTH = 256
 
 
 def as_words(dram_words):
@@ -53,12 +52,12 @@ def tile_picked_scoreput_tanh_po_kernel(
         offs_sb = keep.tile([P, PICKED // 16], U16, name="offs_sb")
         slot_sb = keep.tile([P, PICKED // 16], U16, name="slot_sb")
         d_table = keep.tile([P, TABLE], U32, name="d_table", align_bytes=64)
-        x_table = keep.tile([P, TABLE], U32, name="x_table", tag="x_table", align_bytes=64)
+        x_table = keep.tile([P, TABLE], U32, name="x_table", align_bytes=64)
         d_scale_table = keep.tile([P, TABLE], U8, name="d_scale_table", align_bytes=64)
         x_scale_table = keep.tile([P, TABLE], U8, name="x_scale_table", align_bytes=64)
         gn_sb = keep.tile([P, PACK], F32, name="gn_sb")
-
         w_natural = keep.tile([P, PICKED], U32, name="w_natural", align_bytes=64)
+
         nc.gpsimd.memset(d_scale_table[:].bitcast(I32), 0)
         nc.gpsimd.memset(x_scale_table[:].bitcast(I32), 0)
 
@@ -68,75 +67,64 @@ def tile_picked_scoreput_tanh_po_kernel(
         nc.sync.dma_start(kidx_sb[:], kidx)
         nc.sync.dma_start(offs_sb[:], offs)
         nc.sync.dma_start(d_table[:].bitcast(I32)[:, :FIRST_COLUMNS], d_source[:, :FIRST_COLUMNS])
-        nc.sync.dma_start(d_scale_table[:].bitcast(I32)[0:P:8, :], d_rows)
+        for r in range(2):
+            nc.sync.dma_start(d_scale_table[:].bitcast(I32)[r:P:16, :], d_rows[r:16:2, :])
         nc.sync.dma_start(d_table[:].bitcast(I32)[:, FIRST_COLUMNS:], d_source[:, FIRST_COLUMNS:])
         for r in range(4):
             nc.sync.dma_start(x_scale_table[:].bitcast(I32)[r:P:32, :], x_rows[r:16:4, :])
         nc.sync.dma_start(x_table[:].bitcast(I32), as_words(x_words))
         nc.sync.dma_start(slot_sb[:], slot)
-
-        nc.gpsimd.dma_start(w_natural[:].bitcast(I32), as_words(w1_words))
+        nc.sync.dma_start(w_natural[:].bitcast(I32), as_words(w1_words))
         nc.gpsimd.dma_start(gn_sb[:], gn.rearrange("(p t) o -> p (t o)", t=PACK))
-        windows = {}
-        for t in PLANE_ORDER[:2]:
-            windows[t] = keep.tile([P, SLOTS], F32, name="window%d" % t)
-            nc.vector.memset(windows[t][:], 0.0)
+
+        windows = [keep.tile([P, SLOTS], F32, name="window%d" % i) for i in range(2)]
+        for window in windows:
+            nc.vector.memset(window[:], 0.0)
 
         d_scale_picked = keep.tile([P, PICKED], U8, name="d_scale_picked", tag="picked_bytes", align_bytes=64)
         d_scale_dealt = keep.tile([P, PICKED], U8, name="d_scale_dealt", align_bytes=64)
         nc.vector.tensor_copy(d_scale_picked[:], d_scale_table[:].indirect(kidx_sb[:]))
         deal(nc.vector, d_scale_dealt, d_scale_picked)
-        for r in range(1, 4):
-            queue = nc.sync if r == 2 else nc.scalar
-            queue.dma_start(d_scale_dealt[:].bitcast(I32)[r:P:32, :], d_scale_dealt[:].bitcast(I32)[8 * r : P : 32, :])
+        for r in range(2):
+            nc.scalar.dma_start(d_scale_dealt[:].bitcast(I32)[2 + r : P : 32, :], d_scale_dealt[:].bitcast(I32)[16 + r : P : 32, :])
 
         d_picked = keep.tile([P, PICKED], U32, name="d_picked", align_bytes=64)
         d_dealt = keep.tile([P, PICKED], U32, name="d_dealt", align_bytes=64)
         nc.vector.tensor_copy(d_picked[:], d_table[:].indirect(kidx_sb[:]))
-
-        x_scale_picked = keep.tile([P, PICKED], U8, name="x_scale_picked", align_bytes=64)
-        x_picked = [keep.tile([P, HALF], U32, name="x_picked%d" % h, align_bytes=64) for h in range(2)]
-        nc.vector.tensor_copy(x_scale_picked[:], x_scale_table[:].indirect(offs_sb[:]))
         deal(nc.vector, d_dealt, d_picked)
-        for h in range(2):
-            nc.vector.tensor_copy(x_picked[h][:], x_table[:].indirect(offs_sb[:, h * 16 : (h + 1) * 16]))
 
-        w_dealt = keep.tile([P, PICKED], U32, name="w_dealt", tag="x_table", align_bytes=64)
-        deal(nc.vector, w_dealt, w_natural)
+        x_scale_picked = [keep.tile([P, HALF], U8, name="x_scale_picked%d" % h, align_bytes=64) for h in range(2)]
+        x_picked = [keep.tile([P, HALF], U32, name="x_picked%d" % h, align_bytes=64) for h in range(2)]
+        for h in range(2):
+            entries = offs_sb[:, h * 16 : (h + 1) * 16]
+            nc.vector.tensor_copy(x_scale_picked[h][:], x_scale_table[:].indirect(entries))
+            nc.vector.tensor_copy(x_picked[h][:], x_table[:].indirect(entries))
+
         w_scale_natural = keep.tile([P, PICKED], U8, name="w_scale_natural", tag="picked_bytes", align_bytes=64)
         nc.gpsimd.memset(w_scale_natural[:].bitcast(I32), 0)
         w_rows = w1_scales[0].bitcast(I32)
         for r in range(4):
             nc.sync.dma_start(w_scale_natural[:].bitcast(I32)[r:P:32, :], w_rows[r:16:4, :])
 
-        w_scale_dealt = keep.tile([P, PICKED], U8, name="w_scale_dealt", align_bytes=64)
-        deal(nc.gpsimd, w_scale_dealt, w_scale_natural)
+        first = slice(0, CHUNK_WIDTHS[0])
+        middle = slice(first.stop, UPPER_FROM)
+        z_first = keep.tile([P, first.stop, PACK], BF16, name="z_first", tag="z_first", align_bytes=64)
+        z_rest = keep.tile([P, SLOTS - first.stop, PACK], BF16, name="z_rest", align_bytes=64)
 
-        z = keep.tile([P, SLOTS, PACK], BF16, name="z", align_bytes=64)
-        last_plane = PLANE_ORDER[-1]
-        held_weight = {}
-        for t in (PLANE_ORDER[0], PLANE_ORDER[2]):
-            held_weight[t] = keep.tile([P, 1], F32, name="held_weight%d" % t, tag="weight%d" % t)
-            nc.gpsimd.tensor_copy(out=held_weight[t][:], in_=gn_sb[:, t : t + 1])
-        last_weight = []
-        scalar_weight = keep.tile([P, 1], F32, name="scalar_weight", tag="y0")
-        nc.gpsimd.tensor_copy(out=scalar_weight[:], in_=gn_sb[:, last_plane : last_plane + 1])
+        def z_of(cols):
+            if cols.start < first.stop:
+                return z_first[:, cols, :]
+            return z_rest[:, cols.start - first.stop : cols.stop - first.stop, :]
 
-        def weigh(t, cols, weight, engine):
-            if engine == "scalar":
-                nc.scalar.activation(out=z[:, cols, t], in_=windows[t][:, cols], func=COPY, scale=weight)
-            elif engine == "vector":
-                nc.vector.tensor_scalar(z[:, cols, t], windows[t][:, cols], weight, None, MULT)
-            else:
-                nc.gpsimd.tensor_scalar(z[:, cols, t], windows[t][:, cols], weight, 0.0, MULT, ADD)
+        upper = slice(UPPER_FROM, SLOTS)
 
-        scores = []
         pieces = []
-        for t in PLANE_ORDER:
-            width = HALF if t == PLANE_ORDER[0] else PICKED
+        for place, t in enumerate(PART_ORDER):
+            width = HALF if place == 0 else PICKED
             for j0 in range(0, PICKED, width):
-                pieces.append((t, j0, width))
-        for t, j0, width in pieces:
+                pieces.append((place, t, j0, width))
+        scores = []
+        for place, t, j0, width in pieces:
             keys = slice(t * P, (t + 1) * P)
             bank = psum.tile([P, BANK], F32, name="bank", tag="bank")
             for j in range(j0, j0 + width, HALF):
@@ -145,61 +133,81 @@ def tile_picked_scoreput_tanh_po_kernel(
                     lhsT=d_dealt[:, keys].bitcast(FP8X4),
                     lhsT_scale=d_scale_dealt[:, keys],
                     rhs=x_picked[j // HALF][:].bitcast(FP8X4),
-                    rhs_scale=x_scale_picked[:, j : j + HALF],
+                    rhs_scale=x_scale_picked[j // HALF][:],
                     start=True,
                     stop=True,
                 )
             piece_scores = keep.tile([P, width], F32, name="scores%d_%d" % (t, j0), tag="scores%d_%d" % (t, j0), align_bytes=64)
             scores.append(piece_scores)
             nc.scalar.activation(out=piece_scores[:], in_=bank[:, 0:width], func=TANH, scale=SCORE_SCALE)
-        for (t, j0, width), piece_scores in zip(pieces, scores):
+
+        held_weight = keep.tile([P, 1], F32, name="held_weight", tag="weight")
+        nc.gpsimd.tensor_copy(out=held_weight[:], in_=gn_sb[:, PART_ORDER[-2] : PART_ORDER[-2] + 1])
+        w_dealt = None
+        w_scale_dealt = None
+        for (place, t, j0, width), piece_scores in zip(pieces, scores):
+            window = windows[place % 2]
             entries = slot_sb[:, j0 // 16 : (j0 + width) // 16]
-            nc.vector.tensor_copy(windows[t][:].indirect(entries), piece_scores[:])
-            if j0 + width == PICKED and t != PLANE_ORDER[-1]:
-                place = PLANE_ORDER.index(t)
-                plain = gn_sb[:, t : t + 1]
-                if place == 2:
-                    weigh(t, slice(0, EARLY_SLOTS), plain, "scalar")
-                    weigh(t, slice(EARLY_SLOTS, GPSIMD_FROM), plain, "scalar")
-                else:
-                    weigh(t, slice(0, GPSIMD_FROM), held_weight[t][:] if place == 0 else plain, "scalar")
-                weigh(t, slice(GPSIMD_FROM, SLOTS), held_weight[t][:] if place == 2 else plain, "gpsimd")
-                if place < 2:
-                    later = PLANE_ORDER[place + 2]
-                    windows[later] = keep.tile([P, SLOTS], F32, name="window%d" % later, tag="scores%d_%d" % (t, j0), align_bytes=64)
-                    nc.gpsimd.memset(windows[later][:], 0.0)
-                if t in held_weight:
-                    weight = keep.tile([P, 1], F32, name="last_weight%d" % t, tag="weight%d" % t)
-                    nc.scalar.copy(out=weight[:], in_=gn_sb[:, last_plane : last_plane + 1])
-                    last_weight.append(weight)
+            nc.vector.tensor_copy(window[:].indirect(entries), piece_scores[:])
+            if place == 0 and j0 == 0:
+                w_dealt = keep.tile([P, PICKED], U32, name="w_dealt", tag="scores%d_%d" % (t, j0), align_bytes=64)
+                deal(nc.gpsimd, w_dealt, w_natural)
+            if j0 + width == PICKED and place < PACK - 1:
+                weight = held_weight[:] if place == PACK - 2 else gn_sb[:, t : t + 1]
+                for cols in (first, middle):
+                    nc.scalar.activation(out=z_of(cols)[:, :, t], in_=window[:, cols], func=COPY, scale=weight)
+                nc.gpsimd.tensor_scalar(z_of(upper)[:, :, t], window[:, upper], weight, 0.0, MULT, ADD)
+                if place == 0:
+                    w_scale_dealt = keep.tile([P, PICKED], U8, name="w_scale_dealt", tag="scores%d_%d" % (t, j0), align_bytes=64)
+                    deal(nc.gpsimd, w_scale_dealt, w_scale_natural)
+
+        last = PART_ORDER[-1]
+        window = windows[(PACK - 1) % 2]
+        last_weight = keep.tile([P, 1], F32, name="last_weight", tag="weight")
+        nc.scalar.copy(out=last_weight[:], in_=gn_sb[:, last : last + 1])
+        weight = last_weight[:]
+        scalar_share = slice(SCALAR_FROM, SLOTS)
+        nc.scalar.activation(out=z_of(scalar_share)[:, :, last], in_=window[:, scalar_share], func=COPY, scale=weight)
 
         z_codes = keep.tile([P, SLOTS], U32, name="z_codes", align_bytes=64)
         z_scales = keep.tile([P, SLOTS], U8, name="z_scales", align_bytes=64)
-        chunks = [slice(w0, w0 + width) for w0, width in zip(CHUNK_STARTS, CHUNK_WIDTHS)]
-        for c, cols in enumerate(chunks):
-            if c in SCALAR_CHUNKS:
-                weight = scalar_weight[:]
-            else:
-                weight = last_weight[0 if cols.start < EARLY_SLOTS else 1][:]
-            weigh(last_plane, cols, weight, "scalar" if c in SCALAR_CHUNKS else "vector")
-            if c != len(chunks) - 2:
-                span = slice(chunks[c - 1].start, cols.stop) if c == len(chunks) - 1 else cols
-                nc.vector.quantize_mx(out=z_codes[:, span].bitcast(FP8X4), scales=z_scales[:, span], in_=z[:, span, :].rearrange("p w t -> p (w t)"))
+        chunks = []
+        for width in CHUNK_WIDTHS:
+            start = chunks[-1].stop if chunks else 0
+            chunks.append(slice(start, start + width))
+
+        def weigh_last(cols, weight):
+            nc.vector.tensor_scalar(z_of(cols)[:, :, last], window[:, cols], weight, None, MULT)
+
+        def quantise_z(cols):
+            nc.vector.quantize_mx(out=z_codes[:, cols].bitcast(FP8X4), scales=z_scales[:, cols], in_=z_of(cols).rearrange("p w t -> p (w t)"))
+
+        for cols in chunks[:2]:
+            weigh_last(cols, weight)
+        quantise_z(chunks[0])
+        later_weight = keep.tile([P, 1], F32, name="later_weight", tag="z_first", align_bytes=64)
+        nc.vector.tensor_copy(out=later_weight[:], in_=gn_sb[:, last : last + 1])
+        quantise_z(chunks[1])
+        for cols in (chunks[2], slice(chunks[3].start, SCALAR_FROM)):
+            weigh_last(cols, later_weight[:])
+        for cols in chunks[2:]:
+            quantise_z(cols)
 
         y_codes = keep.tile([P, SLOTS], U32, name="y_codes", align_bytes=64)
         y_scales = keep.tile([P, SLOTS], U8, name="y_scales", align_bytes=64)
+        y_rounded = keep.tile([P, SLOTS, PACK], BF16, name="y_rounded", align_bytes=64)
         out_rows = out_0.rearrange("(p t) w -> p t w", t=PACK)
         out_words = as_words(out_1)
-        stored = 0
-        y_rounded = keep.tile([P, SLOTS, PACK], BF16, name="y_rounded", align_bytes=64)
-        for c, cols in enumerate(chunks):
-            width = CHUNK_WIDTHS[c]
+        y = None
+        y_start = 0
+        banks_done = 0
+        for cols in chunks:
+            width = cols.stop - cols.start
             per_bank = BANK // width
-            if c != len(chunks) - 1:
-                stored_width = 2 * width if c == len(chunks) - 2 else width
-                y_tile = keep.tile([P, PACK, stored_width], F32, name="y%d" % c, tag="y%d" % c)
+            if cols.start % PLANE_WIDTH == 0:
+                y = keep.tile([P, PACK, max(width, PLANE_WIDTH)], F32, name="y%d" % cols.start)
                 y_start = cols.start
-            y = y_tile[:, :, cols.start - y_start : cols.stop - y_start]
+            inside = slice(cols.start - y_start, cols.stop - y_start)
             for t0 in range(0, PACK, per_bank):
                 bank = psum.tile([P, BANK], F32, name="bank", tag="bank")
                 for j in range(per_bank):
@@ -213,21 +221,25 @@ def tile_picked_scoreput_tanh_po_kernel(
                         start=True,
                         stop=True,
                     )
-                planes = slice(t0, t0 + per_bank)
-                nc.scalar.copy(out=y[:, planes, :], in_=bank[:].rearrange("p (t w) -> p t w", t=per_bank))
-                if c != len(chunks) - 2:
-                    nc.sync.dma_start(out_rows[:, planes, y_start : cols.stop], y_tile[:, planes, :])
-            nc.vector.tensor_copy(
-                out=y_rounded[:, cols, :].rearrange("p (b i) t -> p b t i", i=4),
-                in_=y.rearrange("p t (b i) -> p b t i", i=4),
-            )
-            if c != 0:
-                span = slice(0, cols.stop) if c == 1 else cols
-                nc.vector.quantize_mx(out=y_codes[:, span].bitcast(FP8X4), scales=y_scales[:, span], in_=y_rounded[:, span, :].rearrange("p w t -> p (w t)"))
-            if c in CODE_STORES_AFTER:
-                done = slice(stored, cols.stop)
-                nc.sync.dma_start(out_words[:, done], y_codes[:, done].bitcast(I32))
-                stored = cols.stop
+                parts = slice(t0, t0 + per_bank)
+                filled = bank[:].rearrange("p (t w) -> p t w", t=per_bank)
+                if banks_done == VECTOR_BANK:
+                    nc.vector.tensor_copy(out=y[:, parts, inside], in_=filled)
+                else:
+                    nc.scalar.copy(out=y[:, parts, inside], in_=filled)
+                banks_done = banks_done + 1
+                nc.sync.dma_start(out_rows[:, parts, cols], y[:, parts, inside])
+            if cols.stop % PLANE_WIDTH == 0:
+                for w0 in range(y_start, cols.stop, PLANE_WIDTH):
+                    span = slice(w0, w0 + PLANE_WIDTH)
+                    nc.vector.tensor_copy(
+                        out=y_rounded[:, span, :].rearrange("p (b i) t -> p b t i", i=4),
+                        in_=y[:, :, w0 - y_start : w0 - y_start + PLANE_WIDTH].rearrange("p t (b i) -> p b t i", i=4),
+                    )
+                    nc.vector.quantize_mx(out=y_codes[:, span].bitcast(FP8X4), scales=y_scales[:, span], in_=y_rounded[:, span, :].rearrange("p w t -> p (w t)"))
+                    if span.stop != PLANE_WIDTH:
+                        done = slice(0 if span.start == PLANE_WIDTH else span.start, span.stop)
+                        nc.sync.dma_start(out_words[:, done], y_codes[:, done].bitcast(I32))
         out_scale_rows = out_2[0].bitcast(I32)
         for r in range(4):
             queue = nc.sync if r >= 2 else nc.scalar

@@ -46,6 +46,7 @@ def tile_picked_scoreput_tanh_po_kernel(
     nc = tc.nc
     with ExitStack() as ctx:
         keep = ctx.enter_context(tc.tile_pool(name="keep", bufs=1))
+        shared = ctx.enter_context(tc.tile_pool(name="shared", bufs=1))
         psum = ctx.enter_context(tc.psum_pool(name="psum", bufs=8))
 
         kidx_sb = keep.tile([P, PICKED // 16], U16, name="kidx_sb")
@@ -89,16 +90,16 @@ def tile_picked_scoreput_tanh_po_kernel(
             nc.scalar.dma_start(d_scale_dealt[:].bitcast(I32)[2 + r : P : 32, :], d_scale_dealt[:].bitcast(I32)[16 + r : P : 32, :])
 
         d_picked = keep.tile([P, PICKED], U32, name="d_picked", align_bytes=64)
-        d_dealt = keep.tile([P, PICKED], U32, name="d_dealt", align_bytes=64)
         nc.vector.tensor_copy(d_picked[:], d_table[:].indirect(kidx_sb[:]))
-        deal(nc.vector, d_dealt, d_picked)
 
-        x_scale_picked = [keep.tile([P, HALF], U8, name="x_scale_picked%d" % h, align_bytes=64) for h in range(2)]
         x_picked = [keep.tile([P, HALF], U32, name="x_picked%d" % h, align_bytes=64) for h in range(2)]
+        x_scale_picked = [keep.tile([P, HALF], U8, name="x_scale_picked0", align_bytes=64)]
+        token_entries = [offs_sb[:, h * 16 : (h + 1) * 16] for h in range(2)]
+        nc.vector.tensor_copy(x_scale_picked[0][:], x_scale_table[:].indirect(token_entries[0]))
+        d_first = shared.tile([P, P], U32, name="d_first", offset=4 * PICKED + HALF - 4 * P, align_bytes=64)
+        nc.vector.tensor_copy(out=d_first[:], in_=d_picked[:, PART_ORDER[0] : PICKED : PACK])
         for h in range(2):
-            entries = offs_sb[:, h * 16 : (h + 1) * 16]
-            nc.vector.tensor_copy(x_scale_picked[h][:], x_scale_table[:].indirect(entries))
-            nc.vector.tensor_copy(x_picked[h][:], x_table[:].indirect(entries))
+            nc.vector.tensor_copy(x_picked[h][:], x_table[:].indirect(token_entries[h]))
 
         w_scale_natural = keep.tile([P, PICKED], U8, name="w_scale_natural", tag="picked_bytes", align_bytes=64)
         nc.gpsimd.memset(w_scale_natural[:].bitcast(I32), 0)
@@ -118,51 +119,63 @@ def tile_picked_scoreput_tanh_po_kernel(
 
         upper = slice(UPPER_FROM, SLOTS)
 
-        pieces = []
-        for place, t in enumerate(PART_ORDER):
-            width = HALF if place == 0 else PICKED
-            for j0 in range(0, PICKED, width):
-                pieces.append((place, t, j0, width))
-        scores = []
-        for place, t, j0, width in pieces:
-            keys = slice(t * P, (t + 1) * P)
+        def score(keys, key_scales, halves, name):
             bank = psum.tile([P, BANK], F32, name="bank", tag="bank")
-            for j in range(j0, j0 + width, HALF):
+            for i, h in enumerate(halves):
                 nc.tensor.matmul_mx(
-                    out=bank[:, j - j0 : j - j0 + HALF],
-                    lhsT=d_dealt[:, keys].bitcast(FP8X4),
-                    lhsT_scale=d_scale_dealt[:, keys],
-                    rhs=x_picked[j // HALF][:].bitcast(FP8X4),
-                    rhs_scale=x_scale_picked[j // HALF][:],
+                    out=bank[:, i * HALF : (i + 1) * HALF],
+                    lhsT=keys.bitcast(FP8X4),
+                    lhsT_scale=key_scales,
+                    rhs=x_picked[h][:].bitcast(FP8X4),
+                    rhs_scale=x_scale_picked[h][:],
                     start=True,
                     stop=True,
                 )
-            piece_scores = keep.tile([P, width], F32, name="scores%d_%d" % (t, j0), tag="scores%d_%d" % (t, j0), align_bytes=64)
-            scores.append(piece_scores)
+            width = len(halves) * HALF
+            piece_scores = keep.tile([P, width], F32, name=name, tag=name, align_bytes=64)
             nc.scalar.activation(out=piece_scores[:], in_=bank[:, 0:width], func=TANH, scale=SCORE_SCALE)
+            return piece_scores
+
+        pieces = [(0, (0,)), (1, (0,)), (0, (1,)), (1, (1,)), (2, (0, 1)), (3, (0, 1))]
+        scores = []
+        d_dealt = None
+        for i, (place, halves) in enumerate(pieces):
+            keys = slice(PART_ORDER[place] * P, (PART_ORDER[place] + 1) * P)
+            scores.append(score(d_first[:] if i == 0 else d_dealt[:, keys], d_scale_dealt[:, keys], halves, "scores%d" % i))
+            if i == 0:
+                d_dealt = shared.tile([P, PICKED], U32, name="d_dealt", offset=0, align_bytes=64)
+                deal(nc.vector, d_dealt, d_picked)
+                later_scales = shared.tile([P, HALF], U8, name="x_scale_picked1", offset=4 * PICKED, align_bytes=64)
+                nc.vector.tensor_copy(later_scales[:], x_scale_table[:].indirect(token_entries[1]))
+                x_scale_picked.append(later_scales)
 
         held_weight = keep.tile([P, 1], F32, name="held_weight", tag="weight")
         nc.gpsimd.tensor_copy(out=held_weight[:], in_=gn_sb[:, PART_ORDER[-2] : PART_ORDER[-2] + 1])
         w_dealt = None
         w_scale_dealt = None
-        for (place, t, j0, width), piece_scores in zip(pieces, scores):
-            window = windows[place % 2]
-            entries = slot_sb[:, j0 // 16 : (j0 + width) // 16]
-            nc.vector.tensor_copy(window[:].indirect(entries), piece_scores[:])
-            if place == 0 and j0 == 0:
-                w_dealt = keep.tile([P, PICKED], U32, name="w_dealt", tag="scores%d_%d" % (t, j0), align_bytes=64)
+        for i, (place, halves) in enumerate(pieces):
+            t = PART_ORDER[place]
+            window = windows[place % 3]
+            entries = slot_sb[:, halves[0] * 16 : (halves[-1] + 1) * 16]
+            nc.vector.tensor_copy(window[:].indirect(entries), scores[i][:])
+            if i == 0:
+                third = keep.tile([P, SLOTS], F32, name="window2", tag="scores0", align_bytes=64)
+                nc.gpsimd.memset(third[:], 0.0)
+                windows.append(third)
+            if i == 1:
+                w_dealt = keep.tile([P, PICKED], U32, name="w_dealt", tag="scores1", align_bytes=64)
                 deal(nc.gpsimd, w_dealt, w_natural)
-            if j0 + width == PICKED and place < PACK - 1:
+            if halves[-1] == 1 and place < PACK - 1:
                 weight = held_weight[:] if place == PACK - 2 else gn_sb[:, t : t + 1]
                 for cols in (first, middle):
                     nc.scalar.activation(out=z_of(cols)[:, :, t], in_=window[:, cols], func=COPY, scale=weight)
                 nc.gpsimd.tensor_scalar(z_of(upper)[:, :, t], window[:, upper], weight, 0.0, MULT, ADD)
-                if place == 0:
-                    w_scale_dealt = keep.tile([P, PICKED], U8, name="w_scale_dealt", tag="scores%d_%d" % (t, j0), align_bytes=64)
-                    deal(nc.gpsimd, w_scale_dealt, w_scale_natural)
+            if i == 2:
+                w_scale_dealt = keep.tile([P, PICKED], U8, name="w_scale_dealt", tag="scores2", align_bytes=64)
+                deal(nc.gpsimd, w_scale_dealt, w_scale_natural)
 
         last = PART_ORDER[-1]
-        window = windows[(PACK - 1) % 2]
+        window = windows[(PACK - 1) % 3]
         last_weight = keep.tile([P, 1], F32, name="last_weight", tag="weight")
         nc.scalar.copy(out=last_weight[:], in_=gn_sb[:, last : last + 1])
         weight = last_weight[:]

@@ -26,6 +26,8 @@ FLOPS = 2 * 512 * 512 * 512 + 2 * 512 * 512 * 1024
 PART_ORDER = (2, 0, 1, 3)
 UPPER_FROM = 768
 FIRST_COLUMNS = 512
+X_PLANE = 4
+FIRST_TOKENS = 128
 SCALAR_FROM = 640
 CHUNK_WIDTHS = (128, 128, 256, 512)
 VECTOR_BANK = 6
@@ -46,7 +48,6 @@ def tile_picked_scoreput_tanh_po_kernel(
     nc = tc.nc
     with ExitStack() as ctx:
         keep = ctx.enter_context(tc.tile_pool(name="keep", bufs=1))
-        shared = ctx.enter_context(tc.tile_pool(name="shared", bufs=1))
         psum = ctx.enter_context(tc.psum_pool(name="psum", bufs=8))
 
         kidx_sb = keep.tile([P, PICKED // 16], U16, name="kidx_sb")
@@ -72,7 +73,7 @@ def tile_picked_scoreput_tanh_po_kernel(
             nc.sync.dma_start(d_scale_table[:].bitcast(I32)[r:P:16, :], d_rows[r:16:2, :])
         nc.sync.dma_start(d_table[:].bitcast(I32)[:, FIRST_COLUMNS:], d_source[:, FIRST_COLUMNS:])
         for r in range(4):
-            nc.sync.dma_start(x_scale_table[:].bitcast(I32)[r:P:32, :], x_rows[r:16:4, :])
+            nc.sync.dma_start(x_scale_table[:].bitcast(I32)[X_PLANE + r : P : 32, :], x_rows[r:16:4, :])
         nc.sync.dma_start(x_table[:].bitcast(I32), as_words(x_words))
         nc.sync.dma_start(slot_sb[:], slot)
         nc.sync.dma_start(w_natural[:].bitcast(I32), as_words(w1_words))
@@ -91,15 +92,15 @@ def tile_picked_scoreput_tanh_po_kernel(
 
         d_picked = keep.tile([P, PICKED], U32, name="d_picked", align_bytes=64)
         nc.vector.tensor_copy(d_picked[:], d_table[:].indirect(kidx_sb[:]))
+        d_dealt = keep.tile([P, PICKED], U32, name="d_dealt", align_bytes=64)
+        deal(nc.vector, d_dealt, d_picked)
 
+        x_scale_picked = [keep.tile([P, HALF], U8, name="x_scale_picked%d" % h, align_bytes=64) for h in range(2)]
         x_picked = [keep.tile([P, HALF], U32, name="x_picked%d" % h, align_bytes=64) for h in range(2)]
-        x_scale_picked = [keep.tile([P, HALF], U8, name="x_scale_picked0", align_bytes=64)]
-        token_entries = [offs_sb[:, h * 16 : (h + 1) * 16] for h in range(2)]
-        nc.vector.tensor_copy(x_scale_picked[0][:], x_scale_table[:].indirect(token_entries[0]))
-        d_first = shared.tile([P, P], U32, name="d_first", offset=4 * PICKED + HALF - 4 * P, align_bytes=64)
-        nc.vector.tensor_copy(out=d_first[:], in_=d_picked[:, PART_ORDER[0] : PICKED : PACK])
         for h in range(2):
-            nc.vector.tensor_copy(x_picked[h][:], x_table[:].indirect(token_entries[h]))
+            entries = offs_sb[:, h * 16 : (h + 1) * 16]
+            nc.vector.tensor_copy(x_scale_picked[h][:], x_scale_table[:].indirect(entries))
+            nc.vector.tensor_copy(x_picked[h][:], x_table[:].indirect(entries))
 
         w_scale_natural = keep.tile([P, PICKED], U8, name="w_scale_natural", tag="picked_bytes", align_bytes=64)
         nc.gpsimd.memset(w_scale_natural[:].bitcast(I32), 0)
@@ -119,44 +120,46 @@ def tile_picked_scoreput_tanh_po_kernel(
 
         upper = slice(UPPER_FROM, SLOTS)
 
-        def score(keys, key_scales, halves, name):
+        def score(t, tokens, name):
+            keys = slice(t * P, (t + 1) * P)
             bank = psum.tile([P, BANK], F32, name="bank", tag="bank")
-            for i, h in enumerate(halves):
+            j = tokens.start
+            while j < tokens.stop:
+                stop = min(tokens.stop, (j // HALF + 1) * HALF)
+                inside = slice(j % HALF, j % HALF + stop - j)
                 nc.tensor.matmul_mx(
-                    out=bank[:, i * HALF : (i + 1) * HALF],
-                    lhsT=keys.bitcast(FP8X4),
-                    lhsT_scale=key_scales,
-                    rhs=x_picked[h][:].bitcast(FP8X4),
-                    rhs_scale=x_scale_picked[h][:],
+                    out=bank[:, j - tokens.start : stop - tokens.start],
+                    lhsT=d_dealt[:, keys].bitcast(FP8X4),
+                    lhsT_scale=d_scale_dealt[:, keys],
+                    rhs=x_picked[j // HALF][:, inside].bitcast(FP8X4),
+                    rhs_scale=x_scale_picked[j // HALF][X_PLANE:P, inside],
                     start=True,
                     stop=True,
                 )
-            width = len(halves) * HALF
+                j = stop
+            width = tokens.stop - tokens.start
             piece_scores = keep.tile([P, width], F32, name=name, tag=name, align_bytes=64)
             nc.scalar.activation(out=piece_scores[:], in_=bank[:, 0:width], func=TANH, scale=SCORE_SCALE)
             return piece_scores
 
-        pieces = [(0, (0,)), (1, (0,)), (0, (1,)), (1, (1,)), (2, (0, 1)), (3, (0, 1))]
-        scores = []
-        d_dealt = None
-        for i, (place, halves) in enumerate(pieces):
-            keys = slice(PART_ORDER[place] * P, (PART_ORDER[place] + 1) * P)
-            scores.append(score(d_first[:] if i == 0 else d_dealt[:, keys], d_scale_dealt[:, keys], halves, "scores%d" % i))
-            if i == 0:
-                d_dealt = shared.tile([P, PICKED], U32, name="d_dealt", offset=0, align_bytes=64)
-                deal(nc.vector, d_dealt, d_picked)
-                later_scales = shared.tile([P, HALF], U8, name="x_scale_picked1", offset=4 * PICKED, align_bytes=64)
-                nc.vector.tensor_copy(later_scales[:], x_scale_table[:].indirect(token_entries[1]))
-                x_scale_picked.append(later_scales)
+        pieces = [
+            (0, slice(0, FIRST_TOKENS)),
+            (1, slice(0, HALF)),
+            (0, slice(FIRST_TOKENS, PICKED)),
+            (1, slice(HALF, PICKED)),
+            (2, slice(0, PICKED)),
+            (3, slice(0, PICKED)),
+        ]
+        scores = [score(PART_ORDER[place], tokens, "scores%d" % i) for i, (place, tokens) in enumerate(pieces)]
 
         held_weight = keep.tile([P, 1], F32, name="held_weight", tag="weight")
         nc.gpsimd.tensor_copy(out=held_weight[:], in_=gn_sb[:, PART_ORDER[-2] : PART_ORDER[-2] + 1])
         w_dealt = None
         w_scale_dealt = None
-        for i, (place, halves) in enumerate(pieces):
+        for i, (place, tokens) in enumerate(pieces):
             t = PART_ORDER[place]
             window = windows[place % 3]
-            entries = slot_sb[:, halves[0] * 16 : (halves[-1] + 1) * 16]
+            entries = slot_sb[:, tokens.start // 16 : tokens.stop // 16]
             nc.vector.tensor_copy(window[:].indirect(entries), scores[i][:])
             if i == 0:
                 third = keep.tile([P, SLOTS], F32, name="window2", tag="scores0", align_bytes=64)
@@ -165,7 +168,7 @@ def tile_picked_scoreput_tanh_po_kernel(
             if i == 1:
                 w_dealt = keep.tile([P, PICKED], U32, name="w_dealt", tag="scores1", align_bytes=64)
                 deal(nc.gpsimd, w_dealt, w_natural)
-            if halves[-1] == 1 and place < PACK - 1:
+            if tokens.stop == PICKED and place < PACK - 1:
                 weight = held_weight[:] if place == PACK - 2 else gn_sb[:, t : t + 1]
                 for cols in (first, middle):
                     nc.scalar.activation(out=z_of(cols)[:, :, t], in_=window[:, cols], func=COPY, scale=weight)

@@ -28,10 +28,7 @@ UPPER_FROM = 768
 FIRST_COLUMNS = 512
 X_PLANE = 4
 FIRST_TOKENS = 128
-SCALAR_FROM = 640
-CHUNK_WIDTHS = (128, 128, 256, 512)
-VECTOR_BANK = 6
-PLANE_WIDTH = 256
+QUARTER = SLOTS // 4
 
 
 def as_words(dram_words):
@@ -108,16 +105,8 @@ def tile_picked_scoreput_tanh_po_kernel(
         for r in range(4):
             nc.sync.dma_start(w_scale_natural[:].bitcast(I32)[r:P:32, :], w_rows[r:16:4, :])
 
-        first = slice(0, CHUNK_WIDTHS[0])
-        middle = slice(first.stop, UPPER_FROM)
-        z_first = keep.tile([P, first.stop, PACK], BF16, name="z_first", tag="z_first", align_bytes=64)
-        z_rest = keep.tile([P, SLOTS - first.stop, PACK], BF16, name="z_rest", align_bytes=64)
-
-        def z_of(cols):
-            if cols.start < first.stop:
-                return z_first[:, cols, :]
-            return z_rest[:, cols.start - first.stop : cols.stop - first.stop, :]
-
+        z = keep.tile([P, SLOTS, PACK], BF16, name="z", align_bytes=64)
+        lower = slice(0, UPPER_FROM)
         upper = slice(UPPER_FROM, SLOTS)
 
         def score(t, tokens, name):
@@ -152,8 +141,6 @@ def tile_picked_scoreput_tanh_po_kernel(
         ]
         scores = [score(PART_ORDER[place], tokens, "scores%d" % i) for i, (place, tokens) in enumerate(pieces)]
 
-        held_weight = keep.tile([P, 1], F32, name="held_weight", tag="weight")
-        nc.gpsimd.tensor_copy(out=held_weight[:], in_=gn_sb[:, PART_ORDER[-2] : PART_ORDER[-2] + 1])
         w_dealt = None
         w_scale_dealt = None
         for i, (place, tokens) in enumerate(pieces):
@@ -169,93 +156,80 @@ def tile_picked_scoreput_tanh_po_kernel(
                 w_dealt = keep.tile([P, PICKED], U32, name="w_dealt", tag="scores1", align_bytes=64)
                 deal(nc.gpsimd, w_dealt, w_natural)
             if tokens.stop == PICKED and place < PACK - 1:
-                weight = held_weight[:] if place == PACK - 2 else gn_sb[:, t : t + 1]
-                for cols in (first, middle):
-                    nc.scalar.activation(out=z_of(cols)[:, :, t], in_=window[:, cols], func=COPY, scale=weight)
-                nc.gpsimd.tensor_scalar(z_of(upper)[:, :, t], window[:, upper], weight, 0.0, MULT, ADD)
+                weight = gn_sb[:, t : t + 1]
+                nc.scalar.activation(out=z[:, lower, t], in_=window[:, lower], func=COPY, scale=weight)
+                nc.gpsimd.tensor_scalar(z[:, upper, t], window[:, upper], weight, 0.0, MULT, ADD)
             if i == 2:
                 w_scale_dealt = keep.tile([P, PICKED], U8, name="w_scale_dealt", tag="scores2", align_bytes=64)
                 deal(nc.gpsimd, w_scale_dealt, w_scale_natural)
 
         last = PART_ORDER[-1]
         window = windows[(PACK - 1) % 3]
-        last_weight = keep.tile([P, 1], F32, name="last_weight", tag="weight")
-        nc.scalar.copy(out=last_weight[:], in_=gn_sb[:, last : last + 1])
-        weight = last_weight[:]
-        scalar_share = slice(SCALAR_FROM, SLOTS)
-        nc.scalar.activation(out=z_of(scalar_share)[:, :, last], in_=window[:, scalar_share], func=COPY, scale=weight)
+        weight = gn_sb[:, last : last + 1]
+        quarters = [slice(w0, w0 + QUARTER) for w0 in range(0, SLOTS, QUARTER)]
+        halves = [slice(w0, w0 + BANK) for w0 in range(0, SLOTS, BANK)]
+        nc.scalar.activation(out=z[:, halves[1], last], in_=window[:, halves[1]], func=COPY, scale=weight)
+        for cols in quarters[:2]:
+            nc.vector.tensor_scalar(z[:, cols, last], window[:, cols], weight, None, MULT)
 
         z_codes = keep.tile([P, SLOTS], U32, name="z_codes", align_bytes=64)
         z_scales = keep.tile([P, SLOTS], U8, name="z_scales", align_bytes=64)
-        chunks = []
-        for width in CHUNK_WIDTHS:
-            start = chunks[-1].stop if chunks else 0
-            chunks.append(slice(start, start + width))
-
-        def weigh_last(cols, weight):
-            nc.vector.tensor_scalar(z_of(cols)[:, :, last], window[:, cols], weight, None, MULT)
-
-        def quantise_z(cols):
-            nc.vector.quantize_mx(out=z_codes[:, cols].bitcast(FP8X4), scales=z_scales[:, cols], in_=z_of(cols).rearrange("p w t -> p (w t)"))
-
-        for cols in chunks[:2]:
-            weigh_last(cols, weight)
-        quantise_z(chunks[0])
-        later_weight = keep.tile([P, 1], F32, name="later_weight", tag="z_first", align_bytes=64)
-        nc.vector.tensor_copy(out=later_weight[:], in_=gn_sb[:, last : last + 1])
-        quantise_z(chunks[1])
-        for cols in (chunks[2], slice(chunks[3].start, SCALAR_FROM)):
-            weigh_last(cols, later_weight[:])
-        for cols in chunks[2:]:
-            quantise_z(cols)
+        for cols in quarters[:2] + halves[1:]:
+            nc.vector.quantize_mx(out=z_codes[:, cols].bitcast(FP8X4), scales=z_scales[:, cols], in_=z[:, cols, :].rearrange("p w t -> p (w t)"))
 
         y_codes = keep.tile([P, SLOTS], U32, name="y_codes", align_bytes=64)
         y_scales = keep.tile([P, SLOTS], U8, name="y_scales", align_bytes=64)
         y_rounded = keep.tile([P, SLOTS, PACK], BF16, name="y_rounded", align_bytes=64)
         out_rows = out_0.rearrange("(p t) w -> p t w", t=PACK)
         out_words = as_words(out_1)
-        y = None
-        y_start = 0
-        banks_done = 0
-        for cols in chunks:
-            width = cols.stop - cols.start
-            per_bank = BANK // width
-            if cols.start % PLANE_WIDTH == 0:
-                y = keep.tile([P, PACK, max(width, PLANE_WIDTH)], F32, name="y%d" % cols.start)
-                y_start = cols.start
-            inside = slice(cols.start - y_start, cols.stop - y_start)
-            for t0 in range(0, PACK, per_bank):
+        y = [keep.tile([P, PACK, BANK], F32, name="y%d" % h) for h in range(2)]
+
+        def multiply(bank_cols, t, cols):
+            rows = slice(t * P, (t + 1) * P)
+            nc.tensor.matmul_mx(
+                out=bank_cols,
+                lhsT=w_dealt[:, rows].bitcast(FP8X4),
+                lhsT_scale=w_scale_dealt[:, rows],
+                rhs=z_codes[:, cols].bitcast(FP8X4),
+                rhs_scale=z_scales[:, cols],
+                start=True,
+                stop=True,
+            )
+
+        def round_planes(cols):
+            inside = slice(cols.start % BANK, cols.start % BANK + QUARTER)
+            nc.vector.tensor_copy(
+                out=y_rounded[:, cols, :].rearrange("p (b i) t -> p b t i", i=4),
+                in_=y[cols.start // BANK][:, :, inside].rearrange("p t (b i) -> p b t i", i=4),
+            )
+
+        def quantise_planes(cols):
+            nc.vector.quantize_mx(out=y_codes[:, cols].bitcast(FP8X4), scales=y_scales[:, cols], in_=y_rounded[:, cols, :].rearrange("p w t -> p (w t)"))
+
+        for t in range(PACK):
+            bank = psum.tile([P, BANK], F32, name="bank", tag="bank")
+            for cols in quarters[:2] if t == 0 else halves[:1]:
+                multiply(bank[:, cols], t, cols)
+            nc.scalar.copy(out=y[0][:, t, :], in_=bank[:])
+            nc.sync.dma_start(out_rows[:, t, halves[0]], y[0][:, t, :])
+        for cols in quarters[:2]:
+            round_planes(cols)
+        quantise_planes(halves[0])
+        nc.sync.dma_start(out_words[:, halves[0]], y_codes[:, halves[0]].bitcast(I32))
+
+        for t0 in range(0, PACK, 2):
+            parts = slice(t0, t0 + 2)
+            for cols in quarters[2:]:
                 bank = psum.tile([P, BANK], F32, name="bank", tag="bank")
-                for j in range(per_bank):
-                    rows = slice((t0 + j) * P, (t0 + j + 1) * P)
-                    nc.tensor.matmul_mx(
-                        out=bank[:, j * width : (j + 1) * width],
-                        lhsT=w_dealt[:, rows].bitcast(FP8X4),
-                        lhsT_scale=w_scale_dealt[:, rows],
-                        rhs=z_codes[:, cols].bitcast(FP8X4),
-                        rhs_scale=z_scales[:, cols],
-                        start=True,
-                        stop=True,
-                    )
-                parts = slice(t0, t0 + per_bank)
-                filled = bank[:].rearrange("p (t w) -> p t w", t=per_bank)
-                if banks_done == VECTOR_BANK:
-                    nc.vector.tensor_copy(out=y[:, parts, inside], in_=filled)
-                else:
-                    nc.scalar.copy(out=y[:, parts, inside], in_=filled)
-                banks_done = banks_done + 1
-                nc.sync.dma_start(out_rows[:, parts, cols], y[:, parts, inside])
-            if cols.stop % PLANE_WIDTH == 0:
-                for w0 in range(y_start, cols.stop, PLANE_WIDTH):
-                    span = slice(w0, w0 + PLANE_WIDTH)
-                    nc.vector.tensor_copy(
-                        out=y_rounded[:, span, :].rearrange("p (b i) t -> p b t i", i=4),
-                        in_=y[:, :, w0 - y_start : w0 - y_start + PLANE_WIDTH].rearrange("p t (b i) -> p b t i", i=4),
-                    )
-                    nc.vector.quantize_mx(out=y_codes[:, span].bitcast(FP8X4), scales=y_scales[:, span], in_=y_rounded[:, span, :].rearrange("p w t -> p (w t)"))
-                    if span.stop != PLANE_WIDTH:
-                        done = slice(0 if span.start == PLANE_WIDTH else span.start, span.stop)
-                        nc.sync.dma_start(out_words[:, done], y_codes[:, done].bitcast(I32))
+                for j in range(2):
+                    multiply(bank[:, j * QUARTER : (j + 1) * QUARTER], t0 + j, cols)
+                inside = slice(cols.start - BANK, cols.stop - BANK)
+                nc.scalar.copy(out=y[1][:, parts, inside], in_=bank[:].rearrange("p (t w) -> p t w", t=2))
+                if parts.stop == PACK:
+                    round_planes(cols)
+                    quantise_planes(cols)
+            nc.sync.dma_start(out_rows[:, parts, halves[1]], y[1][:, parts, :])
+        nc.sync.dma_start(out_words[:, halves[1]], y_codes[:, halves[1]].bitcast(I32))
         out_scale_rows = out_2[0].bitcast(I32)
         for r in range(4):
             queue = nc.sync if r >= 2 else nc.scalar

@@ -24,7 +24,7 @@ HALF = PICKED // 2
 SCORE_SCALE = 0.0625
 FLOPS = 2 * 512 * 512 * 512 + 2 * 512 * 512 * 1024
 PART_ORDER = (2, 0, 1, 3)
-UPPER_FROM = 768
+UPPER_FROM = 640
 FIRST_COLUMNS = 512
 X_PLANE = 4
 FIRST_TOKENS = 128
@@ -160,8 +160,25 @@ def tile_picked_scoreput_tanh_po_kernel(
                 nc.scalar.activation(out=z[:, lower, t], in_=window[:, lower], func=COPY, scale=weight)
                 nc.gpsimd.tensor_scalar(z[:, upper, t], window[:, upper], weight, 0.0, MULT, ADD)
             if i == 2:
-                w_scale_dealt = keep.tile([P, PICKED], U8, name="w_scale_dealt", tag="scores2", align_bytes=64)
-                deal(nc.gpsimd, w_scale_dealt, w_scale_natural)
+                w_scale_dealt = keep.tile([P, (PACK - 1) * P], U8, name="w_scale_dealt", tag="scores2", align_bytes=64)
+                nc.gpsimd.tensor_copy(
+                    out=w_scale_dealt[:].rearrange("p (t m) -> p m t", t=PACK - 1),
+                    in_=w_scale_natural[:].rearrange("p (m t) -> p m t", t=PACK)[:, :, : PACK - 1],
+                )
+
+        w_scale_last = keep.tile([P, P], U8, name="w_scale_last", tag="scores0", align_bytes=64)
+        nc.gpsimd.tensor_copy(out=w_scale_last[:], in_=w_scale_natural[:].rearrange("p (m t) -> p m t", t=PACK)[:, :, PACK - 1])
+        for i in range(2):
+            idle_bank = psum.tile([P, BANK], F32, name="bank", tag="bank")
+            nc.tensor.matmul_mx(
+                out=idle_bank[:],
+                lhsT=w_dealt[:, (PACK - 1) * P :].bitcast(FP8X4),
+                lhsT_scale=w_scale_last[:],
+                rhs=d_dealt[:].bitcast(FP8X4),
+                rhs_scale=d_scale_dealt[:],
+                start=True,
+                stop=True,
+            )
 
         last = PART_ORDER[-1]
         window = windows[(PACK - 1) % 3]
@@ -189,16 +206,16 @@ def tile_picked_scoreput_tanh_po_kernel(
             nc.tensor.matmul_mx(
                 out=bank_cols,
                 lhsT=w_dealt[:, rows].bitcast(FP8X4),
-                lhsT_scale=w_scale_dealt[:, rows],
+                lhsT_scale=w_scale_last[:] if t == PACK - 1 else w_scale_dealt[:, rows],
                 rhs=z_codes[:, cols].bitcast(FP8X4),
                 rhs_scale=z_scales[:, cols],
                 start=True,
                 stop=True,
             )
 
-        def round_planes(cols):
+        def round_planes(cols, copy):
             inside = slice(cols.start % BANK, cols.start % BANK + QUARTER)
-            nc.vector.tensor_copy(
+            copy(
                 out=y_rounded[:, cols, :].rearrange("p (b i) t -> p b t i", i=4),
                 in_=y[cols.start // BANK][:, :, inside].rearrange("p t (b i) -> p b t i", i=4),
             )
@@ -210,12 +227,11 @@ def tile_picked_scoreput_tanh_po_kernel(
             bank = psum.tile([P, BANK], F32, name="bank", tag="bank")
             for cols in quarters[:2] if t == 0 else halves[:1]:
                 multiply(bank[:, cols], t, cols)
-            nc.scalar.copy(out=y[0][:, t, :], in_=bank[:])
+            empty = nc.vector.tensor_copy if t % 2 else nc.scalar.copy
+            empty(out=y[0][:, t, :], in_=bank[:])
             nc.sync.dma_start(out_rows[:, t, halves[0]], y[0][:, t, :])
         for cols in quarters[:2]:
-            round_planes(cols)
-        quantise_planes(halves[0])
-        nc.sync.dma_start(out_words[:, halves[0]], y_codes[:, halves[0]].bitcast(I32))
+            round_planes(cols, nc.vector.tensor_copy)
 
         for t0 in range(0, PACK, 2):
             parts = slice(t0, t0 + 2)
@@ -225,11 +241,13 @@ def tile_picked_scoreput_tanh_po_kernel(
                     multiply(bank[:, j * QUARTER : (j + 1) * QUARTER], t0 + j, cols)
                 inside = slice(cols.start - BANK, cols.stop - BANK)
                 nc.scalar.copy(out=y[1][:, parts, inside], in_=bank[:].rearrange("p (t w) -> p t w", t=2))
-                if parts.stop == PACK:
-                    round_planes(cols)
-                    quantise_planes(cols)
             nc.sync.dma_start(out_rows[:, parts, halves[1]], y[1][:, parts, :])
-        nc.sync.dma_start(out_words[:, halves[1]], y_codes[:, halves[1]].bitcast(I32))
+        round_planes(quarters[2], nc.vector.tensor_copy)
+        round_planes(quarters[3], nc.scalar.copy)
+        for cols in halves[:1] + quarters[2:]:
+            quantise_planes(cols)
+        for cols in (slice(0, quarters[3].start), quarters[3]):
+            nc.sync.dma_start(out_words[:, cols], y_codes[:, cols].bitcast(I32))
         out_scale_rows = out_2[0].bitcast(I32)
         for r in range(4):
             queue = nc.sync if r >= 2 else nc.scalar

@@ -24,11 +24,11 @@ HALF = PICKED // 2
 SCORE_SCALE = 0.0625
 FLOPS = 2 * 512 * 512 * 512 + 2 * 512 * 512 * 1024
 PART_ORDER = (2, 0, 1, 3)
-UPPER_FROM = 640
 FIRST_COLUMNS = 512
 X_PLANE = 4
 FIRST_TOKENS = 128
 QUARTER = SLOTS // 4
+SCALAR_WEIGHS_FROM = 384
 
 
 def as_words(dram_words):
@@ -106,8 +106,8 @@ def tile_picked_scoreput_tanh_po_kernel(
             nc.sync.dma_start(w_scale_natural[:].bitcast(I32)[r:P:32, :], w_rows[r:16:4, :])
 
         z = keep.tile([P, SLOTS, PACK], BF16, name="z", align_bytes=64)
-        lower = slice(0, UPPER_FROM)
-        upper = slice(UPPER_FROM, SLOTS)
+        middle = slice(SCALAR_WEIGHS_FROM, 3 * QUARTER)
+        outer = (slice(0, middle.start), slice(middle.stop, SLOTS))
 
         def score(t, tokens, name):
             keys = slice(t * P, (t + 1) * P)
@@ -157,8 +157,9 @@ def tile_picked_scoreput_tanh_po_kernel(
                 deal(nc.gpsimd, w_dealt, w_natural)
             if tokens.stop == PICKED and place < PACK - 1:
                 weight = gn_sb[:, t : t + 1]
-                nc.scalar.activation(out=z[:, lower, t], in_=window[:, lower], func=COPY, scale=weight)
-                nc.gpsimd.tensor_scalar(z[:, upper, t], window[:, upper], weight, 0.0, MULT, ADD)
+                for cols in outer:
+                    nc.scalar.activation(out=z[:, cols, t], in_=window[:, cols], func=COPY, scale=weight)
+                nc.gpsimd.tensor_scalar(z[:, middle, t], window[:, middle], weight, 0.0, MULT, ADD)
             if i == 2:
                 w_scale_dealt = keep.tile([P, (PACK - 1) * P], U8, name="w_scale_dealt", tag="scores2", align_bytes=64)
                 nc.gpsimd.tensor_copy(
@@ -185,14 +186,23 @@ def tile_picked_scoreput_tanh_po_kernel(
         weight = gn_sb[:, last : last + 1]
         quarters = [slice(w0, w0 + QUARTER) for w0 in range(0, SLOTS, QUARTER)]
         halves = [slice(w0, w0 + BANK) for w0 in range(0, SLOTS, BANK)]
-        nc.scalar.activation(out=z[:, halves[1], last], in_=window[:, halves[1]], func=COPY, scale=weight)
-        for cols in quarters[:2]:
-            nc.vector.tensor_scalar(z[:, cols, last], window[:, cols], weight, None, MULT)
-
         z_codes = keep.tile([P, SLOTS], U32, name="z_codes", align_bytes=64)
         z_scales = keep.tile([P, SLOTS], U8, name="z_scales", align_bytes=64)
-        for cols in quarters[:2] + halves[1:]:
+
+        def quantise_z(cols):
             nc.vector.quantize_mx(out=z_codes[:, cols].bitcast(FP8X4), scales=z_scales[:, cols], in_=z[:, cols, :].rearrange("p w t -> p (w t)"))
+
+        for cols in (slice(SCALAR_WEIGHS_FROM, BANK), quarters[2]):
+            nc.scalar.activation(out=z[:, cols, last], in_=window[:, cols], func=COPY, scale=weight)
+        late_weight = keep.tile([P, 1], F32, name="late_weight", tag="scores5", align_bytes=64)
+        nc.scalar.copy(out=late_weight[:], in_=weight)
+        for cols in (quarters[0], slice(QUARTER, SCALAR_WEIGHS_FROM)):
+            nc.vector.tensor_scalar(z[:, cols, last], window[:, cols], weight, None, MULT)
+        for cols in quarters[:2]:
+            quantise_z(cols)
+        nc.vector.tensor_scalar(z[:, quarters[3], last], window[:, quarters[3]], late_weight[:], None, MULT)
+        for cols in quarters[2:]:
+            quantise_z(cols)
 
         y_codes = keep.tile([P, SLOTS], U32, name="y_codes", align_bytes=64)
         y_scales = keep.tile([P, SLOTS], U8, name="y_scales", align_bytes=64)
@@ -223,13 +233,12 @@ def tile_picked_scoreput_tanh_po_kernel(
         def quantise_planes(cols):
             nc.vector.quantize_mx(out=y_codes[:, cols].bitcast(FP8X4), scales=y_scales[:, cols], in_=y_rounded[:, cols, :].rearrange("p w t -> p (w t)"))
 
-        for t in range(PACK):
+        for t, cols in [(0, quarters[0]), (0, quarters[1])] + [(t, halves[0]) for t in range(1, PACK)]:
             bank = psum.tile([P, BANK], F32, name="bank", tag="bank")
-            for cols in quarters[:2] if t == 0 else halves[:1]:
-                multiply(bank[:, cols], t, cols)
+            multiply(bank[:, cols], t, cols)
             empty = nc.vector.tensor_copy if t % 2 else nc.scalar.copy
-            empty(out=y[0][:, t, :], in_=bank[:])
-            nc.sync.dma_start(out_rows[:, t, halves[0]], y[0][:, t, :])
+            empty(out=y[0][:, t, cols], in_=bank[:, cols])
+            nc.sync.dma_start(out_rows[:, t, cols], y[0][:, t, cols])
         for cols in quarters[:2]:
             round_planes(cols, nc.vector.tensor_copy)
 

@@ -28,7 +28,9 @@ FIRST_COLUMNS = 512
 X_PLANE = 4
 FIRST_TOKENS = 128
 QUARTER = SLOTS // 4
-SCALAR_WEIGHS_FROM = 384
+EIGHTH = SLOTS // 8
+SCALAR_ROUNDS_FROM = 832
+GPSIMD_WEIGHS = slice(256, 640)
 
 
 def as_words(dram_words):
@@ -106,7 +108,7 @@ def tile_picked_scoreput_tanh_po_kernel(
             nc.sync.dma_start(w_scale_natural[:].bitcast(I32)[r:P:32, :], w_rows[r:16:4, :])
 
         z = keep.tile([P, SLOTS, PACK], BF16, name="z", align_bytes=64)
-        middle = slice(SCALAR_WEIGHS_FROM, 3 * QUARTER)
+        middle = GPSIMD_WEIGHS
         outer = (slice(0, middle.start), slice(middle.stop, SLOTS))
 
         def score(t, tokens, name):
@@ -192,15 +194,16 @@ def tile_picked_scoreput_tanh_po_kernel(
         def quantise_z(cols):
             nc.vector.quantize_mx(out=z_codes[:, cols].bitcast(FP8X4), scales=z_scales[:, cols], in_=z[:, cols, :].rearrange("p w t -> p (w t)"))
 
-        for cols in (slice(SCALAR_WEIGHS_FROM, BANK), quarters[2]):
-            nc.scalar.activation(out=z[:, cols, last], in_=window[:, cols], func=COPY, scale=weight)
+        eighths = [slice(w0, w0 + EIGHTH) for w0 in range(0, SLOTS, EIGHTH)]
+        nc.scalar.activation(out=z[:, quarters[1], last], in_=window[:, quarters[1]], func=COPY, scale=weight)
         late_weight = keep.tile([P, 1], F32, name="late_weight", tag="scores5", align_bytes=64)
         nc.scalar.copy(out=late_weight[:], in_=weight)
-        for cols in (quarters[0], slice(QUARTER, SCALAR_WEIGHS_FROM)):
+        for cols in eighths[:2]:
             nc.vector.tensor_scalar(z[:, cols, last], window[:, cols], weight, None, MULT)
-        for cols in quarters[:2]:
+        for cols in eighths[:2] + quarters[1:2]:
             quantise_z(cols)
-        nc.vector.tensor_scalar(z[:, quarters[3], last], window[:, quarters[3]], late_weight[:], None, MULT)
+        for cols in quarters[2:]:
+            nc.vector.tensor_scalar(z[:, cols, last], window[:, cols], late_weight[:], None, MULT)
         for cols in quarters[2:]:
             quantise_z(cols)
 
@@ -224,7 +227,7 @@ def tile_picked_scoreput_tanh_po_kernel(
             )
 
         def round_planes(cols, copy):
-            inside = slice(cols.start % BANK, cols.start % BANK + QUARTER)
+            inside = slice(cols.start % BANK, cols.start % BANK + cols.stop - cols.start)
             copy(
                 out=y_rounded[:, cols, :].rearrange("p (b i) t -> p b t i", i=4),
                 in_=y[cols.start // BANK][:, :, inside].rearrange("p t (b i) -> p b t i", i=4),
@@ -233,14 +236,13 @@ def tile_picked_scoreput_tanh_po_kernel(
         def quantise_planes(cols):
             nc.vector.quantize_mx(out=y_codes[:, cols].bitcast(FP8X4), scales=y_scales[:, cols], in_=y_rounded[:, cols, :].rearrange("p w t -> p (w t)"))
 
-        for t, cols in [(0, quarters[0]), (0, quarters[1])] + [(t, halves[0]) for t in range(1, PACK)]:
+        lower = [(0, eighths[0]), (0, eighths[1]), (1, quarters[0]), (1, quarters[1]), (0, quarters[1]), (2, halves[0]), (3, halves[0])]
+        for t, cols in lower:
             bank = psum.tile([P, BANK], F32, name="bank", tag="bank")
             multiply(bank[:, cols], t, cols)
-            empty = nc.vector.tensor_copy if t % 2 else nc.scalar.copy
+            empty = nc.vector.tensor_copy if t == 2 else nc.scalar.copy
             empty(out=y[0][:, t, cols], in_=bank[:, cols])
             nc.sync.dma_start(out_rows[:, t, cols], y[0][:, t, cols])
-        for cols in quarters[:2]:
-            round_planes(cols, nc.vector.tensor_copy)
 
         for t0 in range(0, PACK, 2):
             parts = slice(t0, t0 + 2)
@@ -249,13 +251,17 @@ def tile_picked_scoreput_tanh_po_kernel(
                 for j in range(2):
                     multiply(bank[:, j * QUARTER : (j + 1) * QUARTER], t0 + j, cols)
                 inside = slice(cols.start - BANK, cols.stop - BANK)
-                nc.scalar.copy(out=y[1][:, parts, inside], in_=bank[:].rearrange("p (t w) -> p t w", t=2))
+                empty = nc.vector.tensor_copy if (t0, cols) == (0, quarters[2]) else nc.scalar.copy
+                empty(out=y[1][:, parts, inside], in_=bank[:].rearrange("p (t w) -> p t w", t=2))
             nc.sync.dma_start(out_rows[:, parts, halves[1]], y[1][:, parts, :])
-        round_planes(quarters[2], nc.vector.tensor_copy)
-        round_planes(quarters[3], nc.scalar.copy)
-        for cols in halves[:1] + quarters[2:]:
+        for cols in quarters[:3]:
+            round_planes(cols, nc.vector.tensor_copy)
+        quantise_planes(halves[0])
+        round_planes(slice(quarters[3].start, SCALAR_ROUNDS_FROM), nc.vector.tensor_copy)
+        round_planes(slice(SCALAR_ROUNDS_FROM, SLOTS), nc.scalar.copy)
+        for cols in quarters[2:]:
             quantise_planes(cols)
-        for cols in (slice(0, quarters[3].start), quarters[3]):
+        for cols in halves[:1] + quarters[2:]:
             nc.sync.dma_start(out_words[:, cols], y_codes[:, cols].bitcast(I32))
         out_scale_rows = out_2[0].bitcast(I32)
         for r in range(4):

@@ -54,10 +54,8 @@ def tile_picked_scoreput_tanh_po_kernel(
         slot_sb = keep.tile([P, PICKED // 16], U16, name="slot_sb")
         d_table = keep.tile([P, TABLE], U32, name="d_table", align_bytes=64)
         x_table = keep.tile([P, TABLE], U32, name="x_table", align_bytes=64)
-        d_scale_table = keep.tile([P, TABLE], U8, name="d_scale_table", align_bytes=64)
+        d_scale_table = keep.tile([P, TABLE], U8, name="d_scale_table", tag="d_scale_table", align_bytes=64)
         x_scale_table = keep.tile([P, TABLE], U8, name="x_scale_table", align_bytes=64)
-        gn_sb = keep.tile([P, PACK], F32, name="gn_sb")
-        w_natural = keep.tile([P, PICKED], U32, name="w_natural", align_bytes=64)
 
         nc.gpsimd.memset(d_scale_table[:].bitcast(I32), 0)
         nc.gpsimd.memset(x_scale_table[:].bitcast(I32), 0)
@@ -75,8 +73,6 @@ def tile_picked_scoreput_tanh_po_kernel(
             nc.sync.dma_start(x_scale_table[:].bitcast(I32)[X_PLANE + r : P : 32, :], x_rows[r:16:4, :])
         nc.sync.dma_start(x_table[:].bitcast(I32), as_words(x_words))
         nc.sync.dma_start(slot_sb[:], slot)
-        nc.sync.dma_start(w_natural[:].bitcast(I32), as_words(w1_words))
-        nc.gpsimd.dma_start(gn_sb[:], gn.rearrange("(p t) o -> p (t o)", t=PACK))
 
         windows = [keep.tile([P, SLOTS], F32, name="window%d" % i) for i in range(2)]
         for window in windows:
@@ -89,10 +85,15 @@ def tile_picked_scoreput_tanh_po_kernel(
         for r in range(2):
             nc.scalar.dma_start(d_scale_dealt[:].bitcast(I32)[2 + r : P : 32, :], d_scale_dealt[:].bitcast(I32)[16 + r : P : 32, :])
 
-        d_picked = keep.tile([P, PICKED], U32, name="d_picked", align_bytes=64)
+        gn_sb = keep.tile([P, PACK], F32, name="gn_sb", tag="d_scale_table", align_bytes=64)
+        nc.gpsimd.dma_start(gn_sb[:], gn.rearrange("(p t) o -> p (t o)", t=PACK))
+
+        d_picked = keep.tile([P, PICKED], U32, name="d_picked", tag="picked_words", align_bytes=64)
         nc.vector.tensor_copy(d_picked[:], d_table[:].indirect(kidx_sb[:]))
         d_dealt = keep.tile([P, PICKED], U32, name="d_dealt", align_bytes=64)
         deal(nc.vector, d_dealt, d_picked)
+        w_natural = keep.tile([P, PICKED], U32, name="w_natural", tag="picked_words", align_bytes=64)
+        nc.sync.dma_start(w_natural[:].bitcast(I32), as_words(w1_words))
 
         x_scale_picked = [keep.tile([P, HALF], U8, name="x_scale_picked%d" % h, align_bytes=64) for h in range(2)]
         x_picked = [keep.tile([P, HALF], U32, name="x_picked%d" % h, align_bytes=64) for h in range(2)]
@@ -261,7 +262,7 @@ def tile_picked_scoreput_tanh_po_kernel(
         round_planes(slice(SCALAR_ROUNDS_FROM, SLOTS), nc.scalar.copy)
         for cols in quarters[2:]:
             quantise_planes(cols)
-        for cols in halves[:1] + quarters[2:]:
+        for cols in halves:
             nc.sync.dma_start(out_words[:, cols], y_codes[:, cols].bitcast(I32))
         out_scale_rows = out_2[0].bitcast(I32)
         for r in range(4):

@@ -25,7 +25,7 @@ SCORE_SCALE = 0.0625
 FLOPS = 2 * 512 * 512 * 512 + 2 * 512 * 512 * 1024
 PART_ORDER = (2, 0, 1, 3)
 FIRST_COLUMNS = 512
-X_PLANE = 4
+X_ROWS_FROM = 112
 FIRST_TOKENS = 128
 QUARTER = SLOTS // 4
 EIGHTH = SLOTS // 8
@@ -53,37 +53,48 @@ def tile_picked_scoreput_tanh_po_kernel(
         offs_sb = keep.tile([P, PICKED // 16], U16, name="offs_sb")
         slot_sb = keep.tile([P, PICKED // 16], U16, name="slot_sb")
         d_table = keep.tile([P, TABLE], U32, name="d_table", align_bytes=64)
-        x_table = keep.tile([P, TABLE], U32, name="x_table", align_bytes=64)
+        x_table = keep.tile([P, TABLE], U32, name="x_table", tag="x_table", align_bytes=64)
         d_scale_table = keep.tile([P, TABLE], U8, name="d_scale_table", tag="d_scale_table", align_bytes=64)
-        x_scale_table = keep.tile([P, TABLE], U8, name="x_scale_table", align_bytes=64)
+        x_scale_table = keep.tile([P, TABLE], U8, name="x_scale_table", tag="x_scale_table", align_bytes=64)
 
         nc.gpsimd.memset(d_scale_table[:].bitcast(I32), 0)
-        nc.gpsimd.memset(x_scale_table[:].bitcast(I32), 0)
+        nc.vector.memset(x_scale_table[:X_ROWS_FROM, :].bitcast(I32), 0)
+        x_planes = [keep.tile([P, HALF], U8, name="x_plane%d" % h, align_bytes=64) for h in range(2)]
+        for plane in x_planes:
+            nc.gpsimd.memset(plane[:].bitcast(I32), 0)
 
         d_source = as_words(d_words)
         d_rows = d_scales[0].bitcast(I32)
         x_rows = x_scales[0].bitcast(I32)
-        nc.sync.dma_start(kidx_sb[:], kidx)
         nc.sync.dma_start(offs_sb[:], offs)
+        nc.sync.dma_start(x_scale_table[X_ROWS_FROM:, :].bitcast(I32), x_rows)
+        nc.sync.dma_start(kidx_sb[:], kidx)
         nc.sync.dma_start(d_table[:].bitcast(I32)[:, :FIRST_COLUMNS], d_source[:, :FIRST_COLUMNS])
         for r in range(2):
             nc.sync.dma_start(d_scale_table[:].bitcast(I32)[r:P:16, :], d_rows[r:16:2, :])
         nc.sync.dma_start(d_table[:].bitcast(I32)[:, FIRST_COLUMNS:], d_source[:, FIRST_COLUMNS:])
-        for r in range(4):
-            nc.sync.dma_start(x_scale_table[:].bitcast(I32)[X_PLANE + r : P : 32, :], x_rows[r:16:4, :])
         nc.sync.dma_start(x_table[:].bitcast(I32), as_words(x_words))
         nc.sync.dma_start(slot_sb[:], slot)
 
         windows = [keep.tile([P, SLOTS], F32, name="window%d" % i) for i in range(2)]
-        for window in windows:
-            nc.vector.memset(window[:], 0.0)
+        nc.vector.memset(windows[0][:], 0.0)
+        nc.gpsimd.memset(windows[1][:], 0.0)
+
+        def place_token_scales(h, queue, tag):
+            picked = keep.tile([P, HALF], U8, name="x_scale_picked%d" % h, tag=tag, align_bytes=64)
+            nc.vector.tensor_copy(picked[:], x_scale_table[:].indirect(offs_sb[:, h * 16 : (h + 1) * 16]))
+            for q in range(4):
+                rows = slice(X_ROWS_FROM + 4 * q, X_ROWS_FROM + 4 * q + 4)
+                queue.dma_start(x_planes[h][32 * q : 32 * q + 4, :].bitcast(I32), picked[rows, :].bitcast(I32))
+
+        place_token_scales(0, nc.sync, "first_token_bytes")
 
         d_scale_picked = keep.tile([P, PICKED], U8, name="d_scale_picked", tag="picked_bytes", align_bytes=64)
         d_scale_dealt = keep.tile([P, PICKED], U8, name="d_scale_dealt", align_bytes=64)
         nc.vector.tensor_copy(d_scale_picked[:], d_scale_table[:].indirect(kidx_sb[:]))
         deal(nc.vector, d_scale_dealt, d_scale_picked)
         for r in range(2):
-            nc.scalar.dma_start(d_scale_dealt[:].bitcast(I32)[2 + r : P : 32, :], d_scale_dealt[:].bitcast(I32)[16 + r : P : 32, :])
+            nc.sync.dma_start(d_scale_dealt[:].bitcast(I32)[2 + r : P : 32, :], d_scale_dealt[:].bitcast(I32)[16 + r : P : 32, :])
 
         gn_sb = keep.tile([P, PACK], F32, name="gn_sb", tag="d_scale_table", align_bytes=64)
         nc.gpsimd.dma_start(gn_sb[:], gn.rearrange("(p t) o -> p (t o)", t=PACK))
@@ -92,17 +103,16 @@ def tile_picked_scoreput_tanh_po_kernel(
         nc.vector.tensor_copy(d_picked[:], d_table[:].indirect(kidx_sb[:]))
         d_dealt = keep.tile([P, PICKED], U32, name="d_dealt", align_bytes=64)
         deal(nc.vector, d_dealt, d_picked)
-        w_natural = keep.tile([P, PICKED], U32, name="w_natural", tag="picked_words", align_bytes=64)
+        place_token_scales(1, nc.sync, "picked_bytes")
+        w_natural = keep.tile([P, PICKED], U32, name="w_natural", tag="x_scale_table", align_bytes=64)
         nc.sync.dma_start(w_natural[:].bitcast(I32), as_words(w1_words))
 
-        x_scale_picked = [keep.tile([P, HALF], U8, name="x_scale_picked%d" % h, align_bytes=64) for h in range(2)]
-        x_picked = [keep.tile([P, HALF], U32, name="x_picked%d" % h, align_bytes=64) for h in range(2)]
-        for h in range(2):
-            entries = offs_sb[:, h * 16 : (h + 1) * 16]
-            nc.vector.tensor_copy(x_scale_picked[h][:], x_scale_table[:].indirect(entries))
-            nc.vector.tensor_copy(x_picked[h][:], x_table[:].indirect(entries))
+        x_first = keep.tile([P, FIRST_TOKENS], U32, name="x_first", align_bytes=64)
+        x_rest = keep.tile([P, PICKED - FIRST_TOKENS], U32, name="x_rest", align_bytes=64)
+        nc.vector.tensor_copy(x_first[:], x_table[:].indirect(offs_sb[:, : FIRST_TOKENS // 16]))
+        nc.vector.tensor_copy(x_rest[:], x_table[:].indirect(offs_sb[:, FIRST_TOKENS // 16 :]))
 
-        w_scale_natural = keep.tile([P, PICKED], U8, name="w_scale_natural", tag="picked_bytes", align_bytes=64)
+        w_scale_natural = keep.tile([P, PICKED], U8, name="w_scale_natural", tag="x_table", align_bytes=64)
         nc.gpsimd.memset(w_scale_natural[:].bitcast(I32), 0)
         w_rows = w1_scales[0].bitcast(I32)
         for r in range(4):
@@ -117,14 +127,14 @@ def tile_picked_scoreput_tanh_po_kernel(
             bank = psum.tile([P, BANK], F32, name="bank", tag="bank")
             j = tokens.start
             while j < tokens.stop:
-                stop = min(tokens.stop, (j // HALF + 1) * HALF)
-                inside = slice(j % HALF, j % HALF + stop - j)
+                stop = min(tokens.stop, min(edge for edge in (FIRST_TOKENS, HALF, PICKED) if edge > j))
+                words = x_first[:, j:stop] if j < FIRST_TOKENS else x_rest[:, j - FIRST_TOKENS : stop - FIRST_TOKENS]
                 nc.tensor.matmul_mx(
                     out=bank[:, j - tokens.start : stop - tokens.start],
                     lhsT=d_dealt[:, keys].bitcast(FP8X4),
                     lhsT_scale=d_scale_dealt[:, keys],
-                    rhs=x_picked[j // HALF][:, inside].bitcast(FP8X4),
-                    rhs_scale=x_scale_picked[j // HALF][X_PLANE:P, inside],
+                    rhs=words.bitcast(FP8X4),
+                    rhs_scale=x_planes[j // HALF][:, j % HALF : j % HALF + stop - j],
                     start=True,
                     stop=True,
                 )

@@ -23,7 +23,8 @@ BANK = 512
 HALF = PICKED // 2
 SCORE_SCALE = 0.0625
 FLOPS = 2 * 512 * 512 * 512 + 2 * 512 * 512 * 1024
-PART_ORDER = (2, 0, 1, 3)
+PART_ORDER = (0, 2, 1, 3)
+WINDOW_OF = (0, 1, 2, 1)
 FIRST_COLUMNS = 512
 X_ROWS_FROM = 112
 FIRST_TOKENS = 128
@@ -52,7 +53,7 @@ def tile_picked_scoreput_tanh_po_kernel(
         kidx_sb = keep.tile([P, PICKED // 16], U16, name="kidx_sb")
         offs_sb = keep.tile([P, PICKED // 16], U16, name="offs_sb")
         slot_sb = keep.tile([P, PICKED // 16], U16, name="slot_sb")
-        d_table = keep.tile([P, TABLE], U32, name="d_table", align_bytes=64)
+        d_table = keep.tile([P, TABLE], U32, name="d_table", tag="d_table", align_bytes=64)
         x_table = keep.tile([P, TABLE], U32, name="x_table", tag="x_table", align_bytes=64)
         d_scale_table = keep.tile([P, TABLE], U8, name="d_scale_table", tag="d_scale_table", align_bytes=64)
         x_scale_table = keep.tile([P, TABLE], U8, name="x_scale_table", tag="x_scale_table", align_bytes=64)
@@ -101,9 +102,9 @@ def tile_picked_scoreput_tanh_po_kernel(
 
         d_picked = keep.tile([P, PICKED], U32, name="d_picked", tag="picked_words", align_bytes=64)
         nc.vector.tensor_copy(d_picked[:], d_table[:].indirect(kidx_sb[:]))
+        place_token_scales(1, nc.sync, "d_table")
         d_dealt = keep.tile([P, PICKED], U32, name="d_dealt", align_bytes=64)
         deal(nc.vector, d_dealt, d_picked)
-        place_token_scales(1, nc.sync, "picked_bytes")
         w_natural = keep.tile([P, PICKED], U32, name="w_natural", tag="x_scale_table", align_bytes=64)
         nc.sync.dma_start(w_natural[:].bitcast(I32), as_words(w1_words))
 
@@ -147,8 +148,9 @@ def tile_picked_scoreput_tanh_po_kernel(
         pieces = [
             (0, slice(0, FIRST_TOKENS)),
             (1, slice(0, HALF)),
-            (0, slice(FIRST_TOKENS, PICKED)),
+            (0, slice(FIRST_TOKENS, HALF)),
             (1, slice(HALF, PICKED)),
+            (0, slice(HALF, PICKED)),
             (2, slice(0, PICKED)),
             (3, slice(0, PICKED)),
         ]
@@ -158,7 +160,7 @@ def tile_picked_scoreput_tanh_po_kernel(
         w_scale_dealt = None
         for i, (place, tokens) in enumerate(pieces):
             t = PART_ORDER[place]
-            window = windows[place % 3]
+            window = windows[WINDOW_OF[place]]
             entries = slot_sb[:, tokens.start // 16 : tokens.stop // 16]
             nc.vector.tensor_copy(window[:].indirect(entries), scores[i][:])
             if i == 0:
@@ -173,8 +175,8 @@ def tile_picked_scoreput_tanh_po_kernel(
                 for cols in outer:
                     nc.scalar.activation(out=z[:, cols, t], in_=window[:, cols], func=COPY, scale=weight)
                 nc.gpsimd.tensor_scalar(z[:, middle, t], window[:, middle], weight, 0.0, MULT, ADD)
-            if i == 2:
-                w_scale_dealt = keep.tile([P, (PACK - 1) * P], U8, name="w_scale_dealt", tag="scores2", align_bytes=64)
+            if i == 3:
+                w_scale_dealt = keep.tile([P, (PACK - 1) * P], U8, name="w_scale_dealt", tag="scores3", align_bytes=64)
                 nc.gpsimd.tensor_copy(
                     out=w_scale_dealt[:].rearrange("p (t m) -> p m t", t=PACK - 1),
                     in_=w_scale_natural[:].rearrange("p (m t) -> p m t", t=PACK)[:, :, : PACK - 1],
@@ -195,7 +197,7 @@ def tile_picked_scoreput_tanh_po_kernel(
             )
 
         last = PART_ORDER[-1]
-        window = windows[(PACK - 1) % 3]
+        window = windows[WINDOW_OF[PACK - 1]]
         weight = gn_sb[:, last : last + 1]
         quarters = [slice(w0, w0 + QUARTER) for w0 in range(0, SLOTS, QUARTER)]
         halves = [slice(w0, w0 + BANK) for w0 in range(0, SLOTS, BANK)]
@@ -207,7 +209,7 @@ def tile_picked_scoreput_tanh_po_kernel(
 
         eighths = [slice(w0, w0 + EIGHTH) for w0 in range(0, SLOTS, EIGHTH)]
         nc.scalar.activation(out=z[:, quarters[1], last], in_=window[:, quarters[1]], func=COPY, scale=weight)
-        late_weight = keep.tile([P, 1], F32, name="late_weight", tag="scores5", align_bytes=64)
+        late_weight = keep.tile([P, 1], F32, name="late_weight", tag="scores6", align_bytes=64)
         nc.scalar.copy(out=late_weight[:], in_=weight)
         for cols in eighths[:2]:
             nc.vector.tensor_scalar(z[:, cols, last], window[:, cols], weight, None, MULT)

@@ -67,8 +67,8 @@ def tile_picked_scoreput_tanh_po_kernel(
         d_source = as_words(d_words)
         d_rows = d_scales[0].bitcast(I32)
         x_rows = x_scales[0].bitcast(I32)
-        nc.sync.dma_start(offs_sb[:], offs)
         nc.sync.dma_start(x_scale_table[X_ROWS_FROM:, :].bitcast(I32), x_rows)
+        nc.sync.dma_start(offs_sb[:], offs)
         nc.sync.dma_start(kidx_sb[:], kidx)
         nc.sync.dma_start(d_table[:].bitcast(I32)[:, :FIRST_COLUMNS], d_source[:, :FIRST_COLUMNS])
         for r in range(2):
@@ -90,10 +90,15 @@ def tile_picked_scoreput_tanh_po_kernel(
 
         place_token_scales(0, nc.sync, "first_token_bytes")
 
-        d_scale_picked = keep.tile([P, PICKED], U8, name="d_scale_picked", tag="picked_bytes", align_bytes=64)
+        d_scale_picked = [keep.tile([P, HALF], U8, name="d_scale_picked%d" % h, align_bytes=64) for h in range(2)]
         d_scale_dealt = keep.tile([P, PICKED], U8, name="d_scale_dealt", align_bytes=64)
-        nc.vector.tensor_copy(d_scale_picked[:], d_scale_table[:].indirect(kidx_sb[:]))
-        deal(nc.vector, d_scale_dealt, d_scale_picked)
+        for h in range(2):
+            nc.vector.tensor_copy(d_scale_picked[h][:], d_scale_table[:].indirect(kidx_sb[:, h * 16 : (h + 1) * 16]))
+        for h in range(2):
+            nc.vector.tensor_copy(
+                out=d_scale_dealt[:].rearrange("p (t m) -> p t m", t=PACK)[:, :, h * 64 : (h + 1) * 64],
+                in_=d_scale_picked[h][:].rearrange("p (m t) -> p t m", t=PACK),
+            )
         for r in range(2):
             nc.sync.dma_start(d_scale_dealt[:].bitcast(I32)[2 + r : P : 32, :], d_scale_dealt[:].bitcast(I32)[16 + r : P : 32, :])
 
@@ -168,8 +173,11 @@ def tile_picked_scoreput_tanh_po_kernel(
                 nc.gpsimd.memset(third[:], 0.0)
                 windows.append(third)
             if i == 1:
-                w_dealt = keep.tile([P, PICKED], U32, name="w_dealt", tag="scores1", align_bytes=64)
-                deal(nc.gpsimd, w_dealt, w_natural)
+                w_dealt = keep.tile([P, (PACK - 1) * P], U32, name="w_dealt", tag="scores1", align_bytes=64)
+                nc.gpsimd.tensor_copy(
+                    out=w_dealt[:].rearrange("p (t m) -> p m t", t=PACK - 1),
+                    in_=w_natural[:].rearrange("p (m t) -> p m t", t=PACK)[:, :, : PACK - 1],
+                )
             if tokens.stop == PICKED and place < PACK - 1:
                 weight = gn_sb[:, t : t + 1]
                 for cols in outer:
@@ -182,19 +190,21 @@ def tile_picked_scoreput_tanh_po_kernel(
                     in_=w_scale_natural[:].rearrange("p (m t) -> p m t", t=PACK)[:, :, : PACK - 1],
                 )
 
-        w_scale_last = keep.tile([P, P], U8, name="w_scale_last", tag="scores0", align_bytes=64)
-        nc.gpsimd.tensor_copy(out=w_scale_last[:], in_=w_scale_natural[:].rearrange("p (m t) -> p m t", t=PACK)[:, :, PACK - 1])
-        for i in range(2):
-            idle_bank = psum.tile([P, BANK], F32, name="bank", tag="bank")
-            nc.tensor.matmul_mx(
-                out=idle_bank[:],
-                lhsT=w_dealt[:, (PACK - 1) * P :].bitcast(FP8X4),
-                lhsT_scale=w_scale_last[:],
-                rhs=d_dealt[:].bitcast(FP8X4),
-                rhs_scale=d_scale_dealt[:],
-                start=True,
-                stop=True,
-            )
+        w_tail = keep.tile([P, P + P // 4], U32, name="w_tail", tag="scores0", align_bytes=64)
+        w_last = w_tail[:, :P]
+        w_scale_last = w_tail[:, P:].bitcast(U8)
+        nc.gpsimd.tensor_copy(out=w_scale_last, in_=w_scale_natural[:].rearrange("p (m t) -> p m t", t=PACK)[:, :, PACK - 1])
+        nc.gpsimd.tensor_copy(out=w_last, in_=w_natural[:].rearrange("p (m t) -> p m t", t=PACK)[:, :, PACK - 1])
+        idle_bank = psum.tile([P, BANK], F32, name="bank", tag="bank")
+        nc.tensor.matmul_mx(
+            out=idle_bank[:],
+            lhsT=w_last.bitcast(FP8X4),
+            lhsT_scale=w_scale_last,
+            rhs=d_dealt[:].bitcast(FP8X4),
+            rhs_scale=d_scale_dealt[:],
+            start=True,
+            stop=True,
+        )
 
         last = PART_ORDER[-1]
         window = windows[WINDOW_OF[PACK - 1]]
@@ -231,8 +241,8 @@ def tile_picked_scoreput_tanh_po_kernel(
             rows = slice(t * P, (t + 1) * P)
             nc.tensor.matmul_mx(
                 out=bank_cols,
-                lhsT=w_dealt[:, rows].bitcast(FP8X4),
-                lhsT_scale=w_scale_last[:] if t == PACK - 1 else w_scale_dealt[:, rows],
+                lhsT=(w_last if t == PACK - 1 else w_dealt[:, rows]).bitcast(FP8X4),
+                lhsT_scale=w_scale_last if t == PACK - 1 else w_scale_dealt[:, rows],
                 rhs=z_codes[:, cols].bitcast(FP8X4),
                 rhs_scale=z_scales[:, cols],
                 start=True,

@@ -30,6 +30,8 @@ X_ROWS_FROM = 112
 FIRST_TOKENS = 128
 QUARTER = SLOTS // 4
 EIGHTH = SLOTS // 8
+WARM_PASSES = 4
+WARM_ROWS = 32
 SCALAR_ROUNDS_FROM = 832
 GPSIMD_WEIGHS = slice(256, 640)
 
@@ -190,21 +192,22 @@ def tile_picked_scoreput_tanh_po_kernel(
                     in_=w_scale_natural[:].rearrange("p (m t) -> p m t", t=PACK)[:, :, : PACK - 1],
                 )
 
-        w_tail = keep.tile([P, P + P // 4], U32, name="w_tail", tag="scores0", align_bytes=64)
+        w_tail = keep.tile([P, P + P // 4], U32, name="w_tail", tag="scores5", align_bytes=64)
         w_last = w_tail[:, :P]
         w_scale_last = w_tail[:, P:].bitcast(U8)
         nc.gpsimd.tensor_copy(out=w_scale_last, in_=w_scale_natural[:].rearrange("p (m t) -> p m t", t=PACK)[:, :, PACK - 1])
         nc.gpsimd.tensor_copy(out=w_last, in_=w_natural[:].rearrange("p (m t) -> p m t", t=PACK)[:, :, PACK - 1])
         idle_bank = psum.tile([P, BANK], F32, name="bank", tag="bank")
-        nc.tensor.matmul_mx(
-            out=idle_bank[:],
-            lhsT=w_last.bitcast(FP8X4),
-            lhsT_scale=w_scale_last,
-            rhs=d_dealt[:].bitcast(FP8X4),
-            rhs_scale=d_scale_dealt[:],
-            start=True,
-            stop=True,
-        )
+        for i in range(WARM_PASSES):
+            nc.tensor.matmul_mx(
+                out=idle_bank[:WARM_ROWS, :],
+                lhsT=w_last[:, :WARM_ROWS].bitcast(FP8X4),
+                lhsT_scale=w_scale_last[:, :WARM_ROWS],
+                rhs=d_dealt[:].bitcast(FP8X4),
+                rhs_scale=d_scale_dealt[:],
+                start=True,
+                stop=True,
+            )
 
         last = PART_ORDER[-1]
         window = windows[WINDOW_OF[PACK - 1]]

@@ -90,7 +90,7 @@ def tile_picked_scoreput_tanh_po_kernel(
                 rows = slice(X_ROWS_FROM + 4 * q, X_ROWS_FROM + 4 * q + 4)
                 queue.dma_start(x_planes[h][32 * q : 32 * q + 4, :].bitcast(I32), picked[rows, :].bitcast(I32))
 
-        place_token_scales(0, nc.sync, "first_token_bytes")
+        place_token_scales(0, nc.scalar, "first_token_bytes")
 
         d_scale_picked = [keep.tile([P, HALF], U8, name="d_scale_picked%d" % h, align_bytes=64) for h in range(2)]
         d_scale_dealt = keep.tile([P, PICKED], U8, name="d_scale_dealt", align_bytes=64)
@@ -102,7 +102,7 @@ def tile_picked_scoreput_tanh_po_kernel(
                 in_=d_scale_picked[h][:].rearrange("p (m t) -> p t m", t=PACK),
             )
         for r in range(2):
-            nc.sync.dma_start(d_scale_dealt[:].bitcast(I32)[2 + r : P : 32, :], d_scale_dealt[:].bitcast(I32)[16 + r : P : 32, :])
+            nc.scalar.dma_start(d_scale_dealt[:].bitcast(I32)[2 + r : P : 32, :], d_scale_dealt[:].bitcast(I32)[16 + r : P : 32, :])
 
         gn_sb = keep.tile([P, PACK], F32, name="gn_sb", tag="d_scale_table", align_bytes=64)
         nc.gpsimd.dma_start(gn_sb[:], gn.rearrange("(p t) o -> p (t o)", t=PACK))

@@ -33,7 +33,8 @@ EIGHTH = SLOTS // 8
 WARM_PASSES = 4
 WARM_ROWS = 32
 SCALAR_ROUNDS_FROM = 832
-GPSIMD_WEIGHS = slice(256, 640)
+SCALAR_WEIGHS_FROM = 320
+GPSIMD_WEIGHS = slice(320, 704)
 
 
 def as_words(dram_words):
@@ -221,10 +222,11 @@ def tile_picked_scoreput_tanh_po_kernel(
             nc.vector.quantize_mx(out=z_codes[:, cols].bitcast(FP8X4), scales=z_scales[:, cols], in_=z[:, cols, :].rearrange("p w t -> p (w t)"))
 
         eighths = [slice(w0, w0 + EIGHTH) for w0 in range(0, SLOTS, EIGHTH)]
-        nc.scalar.activation(out=z[:, quarters[1], last], in_=window[:, quarters[1]], func=COPY, scale=weight)
+        by_scalar = slice(SCALAR_WEIGHS_FROM, BANK)
+        nc.scalar.activation(out=z[:, by_scalar, last], in_=window[:, by_scalar], func=COPY, scale=weight)
         late_weight = keep.tile([P, 1], F32, name="late_weight", tag="scores6", align_bytes=64)
         nc.scalar.copy(out=late_weight[:], in_=weight)
-        for cols in eighths[:2]:
+        for cols in (eighths[0], slice(EIGHTH, SCALAR_WEIGHS_FROM)):
             nc.vector.tensor_scalar(z[:, cols, last], window[:, cols], weight, None, MULT)
         for cols in eighths[:2] + quarters[1:2]:
             quantise_z(cols)

@@ -289,8 +289,8 @@ def tile_picked_scoreput_tanh_po_kernel(
         round_planes(slice(SCALAR_ROUNDS_FROM, SLOTS), nc.scalar.copy)
         for cols in quarters[2:]:
             quantise_planes(cols)
-        for cols in halves:
-            nc.sync.dma_start(out_words[:, cols], y_codes[:, cols].bitcast(I32))
+        for cols, queue in zip(halves, (nc.scalar, nc.sync)):
+            queue.dma_start(out_words[:, cols], y_codes[:, cols].bitcast(I32))
         out_scale_rows = out_2[0].bitcast(I32)
         for r in range(4):
             queue = nc.sync if r >= 2 else nc.scalar

@@ -204,8 +204,8 @@ def tile_picked_scoreput_tanh_po_kernel(
                 out=idle_bank[:WARM_ROWS, :],
                 lhsT=w_last[:, :WARM_ROWS].bitcast(FP8X4),
                 lhsT_scale=w_scale_last[:, :WARM_ROWS],
-                rhs=d_dealt[:].bitcast(FP8X4),
-                rhs_scale=d_scale_dealt[:],
+                rhs=w_natural[:].bitcast(FP8X4),
+                rhs_scale=w_scale_natural[:],
                 start=True,
                 stop=True,
             )

@@ -34,7 +34,7 @@ WARM_PASSES = 4
 WARM_ROWS = 32
 SCALAR_ROUNDS_FROM = 832
 SCALAR_WEIGHS_FROM = 320
-GPSIMD_WEIGHS = slice(320, 704)
+GPSIMD_WEIGHS = slice(320, 576)
 
 
 def as_words(dram_words):

@@ -105,9 +105,6 @@ def tile_picked_scoreput_tanh_po_kernel(
         for r in range(2):
             nc.scalar.dma_start(d_scale_dealt[:].bitcast(I32)[2 + r : P : 32, :], d_scale_dealt[:].bitcast(I32)[16 + r : P : 32, :])
 
-        gn_sb = keep.tile([P, PACK], F32, name="gn_sb", tag="d_scale_table", align_bytes=64)
-        nc.gpsimd.dma_start(gn_sb[:], gn.rearrange("(p t) o -> p (t o)", t=PACK))
-
         d_picked = keep.tile([P, PICKED], U32, name="d_picked", tag="picked_words", align_bytes=64)
         nc.vector.tensor_copy(d_picked[:], d_table[:].indirect(kidx_sb[:]))
         place_token_scales(1, nc.sync, "d_table")
@@ -115,6 +112,9 @@ def tile_picked_scoreput_tanh_po_kernel(
         deal(nc.vector, d_dealt, d_picked)
         w_natural = keep.tile([P, PICKED], U32, name="w_natural", tag="x_scale_table", align_bytes=64)
         nc.sync.dma_start(w_natural[:].bitcast(I32), as_words(w1_words))
+
+        gn_sb = keep.tile([P, PACK], F32, name="gn_sb", tag="picked_words", align_bytes=64)
+        nc.sync.dma_start(gn_sb[:], gn.rearrange("(p t) o -> p (t o)", t=PACK))
 
         x_first = keep.tile([P, FIRST_TOKENS], U32, name="x_first", align_bytes=64)
         x_rest = keep.tile([P, PICKED - FIRST_TOKENS], U32, name="x_rest", align_bytes=64)

@@ -25,7 +25,7 @@ SCORE_SCALE = 0.0625
 FLOPS = 2 * 512 * 512 * 512 + 2 * 512 * 512 * 1024
 PART_ORDER = (0, 2, 1, 3)
 WINDOW_OF = (0, 1, 2, 1)
-FIRST_COLUMNS = 512
+FIRST_COLUMNS = 640
 X_ROWS_FROM = 112
 FIRST_TOKENS = 128
 QUARTER = SLOTS // 4
@@ -70,10 +70,10 @@ def tile_picked_scoreput_tanh_po_kernel(
         d_source = as_words(d_words)
         d_rows = d_scales[0].bitcast(I32)
         x_rows = x_scales[0].bitcast(I32)
-        nc.sync.dma_start(x_scale_table[X_ROWS_FROM:, :].bitcast(I32), x_rows)
+        nc.scalar.dma_start(x_scale_table[X_ROWS_FROM:, :].bitcast(I32), x_rows)
         nc.sync.dma_start(offs_sb[:], offs)
-        nc.sync.dma_start(kidx_sb[:], kidx)
         nc.sync.dma_start(d_table[:].bitcast(I32)[:, :FIRST_COLUMNS], d_source[:, :FIRST_COLUMNS])
+        nc.sync.dma_start(kidx_sb[:], kidx)
         for r in range(2):
             nc.sync.dma_start(d_scale_table[:].bitcast(I32)[r:P:16, :], d_rows[r:16:2, :])
         nc.sync.dma_start(d_table[:].bitcast(I32)[:, FIRST_COLUMNS:], d_source[:, FIRST_COLUMNS:])

@@ -293,5 +293,4 @@ def tile_picked_scoreput_tanh_po_kernel(
             queue.dma_start(out_words[:, cols], y_codes[:, cols].bitcast(I32))
         out_scale_rows = out_2[0].bitcast(I32)
         for r in range(4):
-            queue = nc.sync if r >= 2 else nc.scalar
-            queue.dma_start(out_scale_rows[r:16:4, :], y_scales[:].bitcast(I32)[r:P:32, :])
+            nc.scalar.dma_start(out_scale_rows[r:16:4, :], y_scales[:].bitcast(I32)[r:P:32, :])

from contextlib import ExitStack

import concourse.mybir as mybir

F32 = mybir.dt.float32
BF16 = mybir.dt.bfloat16
I32 = mybir.dt.int32
U32 = mybir.dt.uint32
U16 = mybir.dt.uint16
U8 = mybir.dt.uint8
FP8X4 = mybir.dt.float8_e4m3fn_x4
TANH = mybir.ActivationFunctionType.Tanh
COPY = mybir.ActivationFunctionType.Copy
MULT = mybir.AluOpType.mult
ADD = mybir.AluOpType.add

P = 128
PACK = 4
TABLE = 2048
PICKED = 512
SLOTS = 1024
BANK = 512
HALF = PICKED // 2
SCORE_SCALE = 0.0625
FLOPS = 2 * 512 * 512 * 512 + 2 * 512 * 512 * 1024
PART_ORDER = (0, 2, 1, 3)
WINDOW_OF = (0, 1, 2, 1)
FIRST_COLUMNS = 640
X_ROWS_FROM = 112
FIRST_TOKENS = 128
QUARTER = SLOTS // 4
EIGHTH = SLOTS // 8
WARM_PASSES = 4
WARM_ROWS = 32
SCALAR_ROUNDS_FROM = 832
SCALAR_WEIGHS_FROM = 320
GPSIMD_WEIGHS = slice(320, 576)


def as_words(dram_words):
    return dram_words[0].rearrange("p n t -> p (n t)").bitcast(I32)


def deal(engine, dealt, natural):
    engine.tensor_copy(out=dealt[:].rearrange("p (t m) -> p m t", t=PACK), in_=natural[:].rearrange("p (m t) -> p m t", t=PACK))


def tile_picked_scoreput_tanh_po_kernel(
    tc, x_words, x_scales, d_words, d_scales, gn, w1_words, w1_scales, offs, kidx, slot, out_0, out_1, out_2
):
    nc = tc.nc
    with ExitStack() as ctx:
        keep = ctx.enter_context(tc.tile_pool(name="keep", bufs=1))
        psum = ctx.enter_context(tc.psum_pool(name="psum", bufs=8))

        kidx_sb = keep.tile([P, PICKED // 16], U16, name="kidx_sb")
        offs_sb = keep.tile([P, PICKED // 16], U16, name="offs_sb")
        slot_sb = keep.tile([P, PICKED // 16], U16, name="slot_sb")
        d_table = keep.tile([P, TABLE], U32, name="d_table", tag="d_table", align_bytes=64)
        x_table = keep.tile([P, TABLE], U32, name="x_table", tag="x_table", align_bytes=64)
        d_scale_table = keep.tile([P, TABLE], U8, name="d_scale_table", tag="d_scale_table", align_bytes=64)
        x_scale_table = keep.tile([P, TABLE], U8, name="x_scale_table", tag="x_scale_table", align_bytes=64)

        nc.gpsimd.memset(d_scale_table[:].bitcast(I32), 0)
        nc.vector.memset(x_scale_table[:X_ROWS_FROM, :].bitcast(I32), 0)
        x_planes = [keep.tile([P, HALF], U8, name="x_plane%d" % h, align_bytes=64) for h in range(2)]
        for plane in x_planes:
            nc.gpsimd.memset(plane[:].bitcast(I32), 0)

        d_source = as_words(d_words)
        d_rows = d_scales[0].bitcast(I32)
        x_rows = x_scales[0].bitcast(I32)
        nc.scalar.dma_start(x_scale_table[X_ROWS_FROM:, :].bitcast(I32), x_rows)
        nc.sync.dma_start(offs_sb[:], offs)
        nc.sync.dma_start(d_table[:].bitcast(I32)[:, :FIRST_COLUMNS], d_source[:, :FIRST_COLUMNS])
        nc.sync.dma_start(kidx_sb[:], kidx)
        for r in range(2):
            nc.sync.dma_start(d_scale_table[:].bitcast(I32)[r:P:16, :], d_rows[r:16:2, :])
        nc.sync.dma_start(d_table[:].bitcast(I32)[:, FIRST_COLUMNS:], d_source[:, FIRST_COLUMNS:])
        nc.sync.dma_start(x_table[:].bitcast(I32), as_words(x_words))
        nc.sync.dma_start(slot_sb[:], slot)

        windows = [keep.tile([P, SLOTS], F32, name="window%d" % i) for i in range(2)]
        nc.vector.memset(windows[0][:], 0.0)
        nc.gpsimd.memset(windows[1][:], 0.0)

        def place_token_scales(h, queue, tag):
            picked = keep.tile([P, HALF], U8, name="x_scale_picked%d" % h, tag=tag, align_bytes=64)
            nc.vector.tensor_copy(picked[:], x_scale_table[:].indirect(offs_sb[:, h * 16 : (h + 1) * 16]))
            for q in range(4):
                rows = slice(X_ROWS_FROM + 4 * q, X_ROWS_FROM + 4 * q + 4)
                queue.dma_start(x_planes[h][32 * q : 32 * q + 4, :].bitcast(I32), picked[rows, :].bitcast(I32))

        place_token_scales(0, nc.scalar, "first_token_bytes")

        d_scale_picked = [keep.tile([P, HALF], U8, name="d_scale_picked%d" % h, align_bytes=64) for h in range(2)]
        d_scale_dealt = keep.tile([P, PICKED], U8, name="d_scale_dealt", align_bytes=64)
        for h in range(2):
            nc.vector.tensor_copy(d_scale_picked[h][:], d_scale_table[:].indirect(kidx_sb[:, h * 16 : (h + 1) * 16]))
        for h in range(2):
            nc.vector.tensor_copy(
                out=d_scale_dealt[:].rearrange("p (t m) -> p t m", t=PACK)[:, :, h * 64 : (h + 1) * 64],
                in_=d_scale_picked[h][:].rearrange("p (m t) -> p t m", t=PACK),
            )
        for r in range(2):
            nc.scalar.dma_start(d_scale_dealt[:].bitcast(I32)[2 + r : P : 32, :], d_scale_dealt[:].bitcast(I32)[16 + r : P : 32, :])

        d_picked = keep.tile([P, PICKED], U32, name="d_picked", tag="picked_words", align_bytes=64)
        nc.vector.tensor_copy(d_picked[:], d_table[:].indirect(kidx_sb[:]))
        place_token_scales(1, nc.sync, "d_table")
        d_dealt = keep.tile([P, PICKED], U32, name="d_dealt", align_bytes=64)
        deal(nc.vector, d_dealt, d_picked)
        w_natural = keep.tile([P, PICKED], U32, name="w_natural", tag="x_scale_table", align_bytes=64)
        nc.sync.dma_start(w_natural[:].bitcast(I32), as_words(w1_words))

        gn_sb = keep.tile([P, PACK], F32, name="gn_sb", tag="picked_words", align_bytes=64)
        nc.sync.dma_start(gn_sb[:], gn.rearrange("(p t) o -> p (t o)", t=PACK))

        x_first = keep.tile([P, FIRST_TOKENS], U32, name="x_first", align_bytes=64)
        x_rest = keep.tile([P, PICKED - FIRST_TOKENS], U32, name="x_rest", align_bytes=64)
        nc.vector.tensor_copy(x_first[:], x_table[:].indirect(offs_sb[:, : FIRST_TOKENS // 16]))
        nc.vector.tensor_copy(x_rest[:], x_table[:].indirect(offs_sb[:, FIRST_TOKENS // 16 :]))

        w_scale_natural = keep.tile([P, PICKED], U8, name="w_scale_natural", tag="x_table", align_bytes=64)
        nc.gpsimd.memset(w_scale_natural[:].bitcast(I32), 0)
        w_rows = w1_scales[0].bitcast(I32)
        for r in range(4):
            nc.sync.dma_start(w_scale_natural[:].bitcast(I32)[r:P:32, :], w_rows[r:16:4, :])

        z = keep.tile([P, SLOTS, PACK], BF16, name="z", align_bytes=64)
        middle = GPSIMD_WEIGHS
        outer = (slice(0, middle.start), slice(middle.stop, SLOTS))

        def score(t, tokens, name):
            keys = slice(t * P, (t + 1) * P)
            bank = psum.tile([P, BANK], F32, name="bank", tag="bank")
            j = tokens.start
            while j < tokens.stop:
                stop = min(tokens.stop, min(edge for edge in (FIRST_TOKENS, HALF, PICKED) if edge > j))
                words = x_first[:, j:stop] if j < FIRST_TOKENS else x_rest[:, j - FIRST_TOKENS : stop - FIRST_TOKENS]
                nc.tensor.matmul_mx(
                    out=bank[:, j - tokens.start : stop - tokens.start],
                    lhsT=d_dealt[:, keys].bitcast(FP8X4),
                    lhsT_scale=d_scale_dealt[:, keys],
                    rhs=words.bitcast(FP8X4),
                    rhs_scale=x_planes[j // HALF][:, j % HALF : j % HALF + stop - j],
                    start=True,
                    stop=True,
                )
                j = stop
            width = tokens.stop - tokens.start
            piece_scores = keep.tile([P, width], F32, name=name, tag=name, align_bytes=64)
            nc.scalar.activation(out=piece_scores[:], in_=bank[:, 0:width], func=TANH, scale=SCORE_SCALE)
            return piece_scores

        pieces = [
            (0, slice(0, FIRST_TOKENS)),
            (1, slice(0, HALF)),
            (0, slice(FIRST_TOKENS, HALF)),
            (1, slice(HALF, PICKED)),
            (0, slice(HALF, PICKED)),
            (2, slice(0, PICKED)),
            (3, slice(0, PICKED)),
        ]
        scores = [score(PART_ORDER[place], tokens, "scores%d" % i) for i, (place, tokens) in enumerate(pieces)]

        w_dealt = None
        w_scale_dealt = None
        for i, (place, tokens) in enumerate(pieces):
            t = PART_ORDER[place]
            window = windows[WINDOW_OF[place]]
            entries = slot_sb[:, tokens.start // 16 : tokens.stop // 16]
            nc.vector.tensor_copy(window[:].indirect(entries), scores[i][:])
            if i == 0:
                third = keep.tile([P, SLOTS], F32, name="window2", tag="scores0", align_bytes=64)
                nc.gpsimd.memset(third[:], 0.0)
                windows.append(third)
            if i == 1:
                w_dealt = keep.tile([P, (PACK - 1) * P], U32, name="w_dealt", tag="scores1", align_bytes=64)
                nc.gpsimd.tensor_copy(
                    out=w_dealt[:].rearrange("p (t m) -> p m t", t=PACK - 1),
                    in_=w_natural[:].rearrange("p (m t) -> p m t", t=PACK)[:, :, : PACK - 1],
                )
            if tokens.stop == PICKED and place < PACK - 1:
                weight = gn_sb[:, t : t + 1]
                for cols in outer:
                    nc.scalar.activation(out=z[:, cols, t], in_=window[:, cols], func=COPY, scale=weight)
                nc.gpsimd.tensor_scalar(z[:, middle, t], window[:, middle], weight, 0.0, MULT, ADD)
            if i == 3:
                w_scale_dealt = keep.tile([P, (PACK - 1) * P], U8, name="w_scale_dealt", tag="scores3", align_bytes=64)
                nc.gpsimd.tensor_copy(
                    out=w_scale_dealt[:].rearrange("p (t m) -> p m t", t=PACK - 1),
                    in_=w_scale_natural[:].rearrange("p (m t) -> p m t", t=PACK)[:, :, : PACK - 1],
                )

        w_tail = keep.tile([P, P + P // 4], U32, name="w_tail", tag="scores5", align_bytes=64)
        w_last = w_tail[:, :P]
        w_scale_last = w_tail[:, P:].bitcast(U8)
        nc.gpsimd.tensor_copy(out=w_scale_last, in_=w_scale_natural[:].rearrange("p (m t) -> p m t", t=PACK)[:, :, PACK - 1])
        nc.gpsimd.tensor_copy(out=w_last, in_=w_natural[:].rearrange("p (m t) -> p m t", t=PACK)[:, :, PACK - 1])
        idle_bank = psum.tile([P, BANK], F32, name="bank", tag="bank")
        for i in range(WARM_PASSES):
            nc.tensor.matmul_mx(
                out=idle_bank[:WARM_ROWS, :],
                lhsT=w_last[:, :WARM_ROWS].bitcast(FP8X4),
                lhsT_scale=w_scale_last[:, :WARM_ROWS],
                rhs=w_natural[:].bitcast(FP8X4),
                rhs_scale=w_scale_natural[:],
                start=True,
                stop=True,
            )

        last = PART_ORDER[-1]
        window = windows[WINDOW_OF[PACK - 1]]
        weight = gn_sb[:, last : last + 1]
        quarters = [slice(w0, w0 + QUARTER) for w0 in range(0, SLOTS, QUARTER)]
        halves = [slice(w0, w0 + BANK) for w0 in range(0, SLOTS, BANK)]
        z_codes = keep.tile([P, SLOTS], U32, name="z_codes", align_bytes=64)
        z_scales = keep.tile([P, SLOTS], U8, name="z_scales", align_bytes=64)

        def quantise_z(cols):
            nc.vector.quantize_mx(out=z_codes[:, cols].bitcast(FP8X4), scales=z_scales[:, cols], in_=z[:, cols, :].rearrange("p w t -> p (w t)"))

        eighths = [slice(w0, w0 + EIGHTH) for w0 in range(0, SLOTS, EIGHTH)]
        by_scalar = slice(SCALAR_WEIGHS_FROM, BANK)
        nc.scalar.activation(out=z[:, by_scalar, last], in_=window[:, by_scalar], func=COPY, scale=weight)
        late_weight = keep.tile([P, 1], F32, name="late_weight", tag="scores6", align_bytes=64)
        nc.scalar.copy(out=late_weight[:], in_=weight)
        for cols in (eighths[0], slice(EIGHTH, SCALAR_WEIGHS_FROM)):
            nc.vector.tensor_scalar(z[:, cols, last], window[:, cols], weight, None, MULT)
        for cols in eighths[:2] + quarters[1:2]:
            quantise_z(cols)
        for cols in quarters[2:]:
            nc.vector.tensor_scalar(z[:, cols, last], window[:, cols], late_weight[:], None, MULT)
        for cols in quarters[2:]:
            quantise_z(cols)

        y_codes = keep.tile([P, SLOTS], U32, name="y_codes", align_bytes=64)
        y_scales = keep.tile([P, SLOTS], U8, name="y_scales", align_bytes=64)
        y_rounded = keep.tile([P, SLOTS, PACK], BF16, name="y_rounded", align_bytes=64)
        out_rows = out_0.rearrange("(p t) w -> p t w", t=PACK)
        out_words = as_words(out_1)
        y = [keep.tile([P, PACK, BANK], F32, name="y%d" % h) for h in range(2)]

        def multiply(bank_cols, t, cols):
            rows = slice(t * P, (t + 1) * P)
            nc.tensor.matmul_mx(
                out=bank_cols,
                lhsT=(w_last if t == PACK - 1 else w_dealt[:, rows]).bitcast(FP8X4),
                lhsT_scale=w_scale_last if t == PACK - 1 else w_scale_dealt[:, rows],
                rhs=z_codes[:, cols].bitcast(FP8X4),
                rhs_scale=z_scales[:, cols],
                start=True,
                stop=True,
            )

        def round_planes(cols, copy):
            inside = slice(cols.start % BANK, cols.start % BANK + cols.stop - cols.start)
            copy(
                out=y_rounded[:, cols, :].rearrange("p (b i) t -> p b t i", i=4),
                in_=y[cols.start // BANK][:, :, inside].rearrange("p t (b i) -> p b t i", i=4),
            )

        def quantise_planes(cols):
            nc.vector.quantize_mx(out=y_codes[:, cols].bitcast(FP8X4), scales=y_scales[:, cols], in_=y_rounded[:, cols, :].rearrange("p w t -> p (w t)"))

        lower = [(0, eighths[0]), (0, eighths[1]), (1, quarters[0]), (1, quarters[1]), (0, quarters[1]), (2, halves[0]), (3, halves[0])]
        for t, cols in lower:
            bank = psum.tile([P, BANK], F32, name="bank", tag="bank")
            multiply(bank[:, cols], t, cols)
            empty = nc.vector.tensor_copy if t == 2 else nc.scalar.copy
            empty(out=y[0][:, t, cols], in_=bank[:, cols])
            nc.sync.dma_start(out_rows[:, t, cols], y[0][:, t, cols])

        for t0 in range(0, PACK, 2):
            parts = slice(t0, t0 + 2)
            for cols in quarters[2:]:
                bank = psum.tile([P, BANK], F32, name="bank", tag="bank")
                for j in range(2):
                    multiply(bank[:, j * QUARTER : (j + 1) * QUARTER], t0 + j, cols)
                inside = slice(cols.start - BANK, cols.stop - BANK)
                empty = nc.vector.tensor_copy if (t0, cols) == (0, quarters[2]) else nc.scalar.copy
                empty(out=y[1][:, parts, inside], in_=bank[:].rearrange("p (t w) -> p t w", t=2))
            nc.sync.dma_start(out_rows[:, parts, halves[1]], y[1][:, parts, :])
        for cols in quarters[:3]:
            round_planes(cols, nc.vector.tensor_copy)
        quantise_planes(halves[0])
        round_planes(slice(quarters[3].start, SCALAR_ROUNDS_FROM), nc.vector.tensor_copy)
        round_planes(slice(SCALAR_ROUNDS_FROM, SLOTS), nc.scalar.copy)
        for cols in quarters[2:]:
            quantise_planes(cols)
        for cols, queue in zip(halves, (nc.scalar, nc.sync)):
            queue.dma_start(out_words[:, cols], y_codes[:, cols].bitcast(I32))
        out_scale_rows = out_2[0].bitcast(I32)
        for r in range(4):
            nc.scalar.dma_start(out_scale_rows[r:16:4, :], y_scales[:].bitcast(I32)[r:P:32, :])
